import numpy as np, ml_dtypes
CORES = [40,64,80,88,96,104,120,144]
N = 8
BF = ml_dtypes.bfloat16
def gentries(a):
    return np.ascontiguousarray(a.reshape(8, 16, -1).transpose(0, 2, 1)).reshape(8, -1)
def gtable(e):
    e = np.asarray(e); return np.ascontiguousarray(e.reshape(8, -1, 16).transpose(0, 2, 1)).reshape(128, -1).astype(np.int32)
W, T, Z, VI, SH = 2048, 128, 3, 6, 4
STEP = (0, 1, 3, 4)
kk = np.arange(16)
def parts(rng):
    return rng.integers(0, 64, (N, 8, 16, W)), rng.integers(0, W, (N, 8, 4, T, 16)), rng.integers(450, 850, (N, 8, 16))
def pack(x, h, th):
    return {"x": np.ascontiguousarray(x.reshape(N, 128, W)).astype(np.float32).astype(BF), "hom": np.stack([gtable(a.reshape(8, -1)) for a in h]),
            "th": np.ascontiguousarray(th.reshape(N, 128, 1)).astype(np.int32)}
def lay(z, u, v):
    z, u, v = np.broadcast_arrays(z, u, v); s = np.arange(4)[:, None, None]
    return np.where((s == 0) | (s == z[..., None, :, :] + 1), u[..., None, :, :], v[..., None, :, :])
def setup_inputs(rng):
    return pack(*parts(rng))
def setup_inputs_spread(rng):
    x, h, th = parts(rng)
    x = (64 * np.exp2(-rng.integers(0, 7, (N, 8, 1, W))) * rng.random((N, 8, 16, W))).astype(np.int64)
    h = (W * rng.random((N, 8, 4, T, 16)) ** rng.integers(1, 5, (N, 8, 1, 1, 1))).astype(np.int64)
    th = (2017 * rng.random((N, 8, 16)) ** 3).astype(np.int64)
    return pack(x, np.minimum(h, W - 1), np.minimum(th, 2016))
def setup_inputs_ends(rng):
    x = 63 * rng.integers(0, 2, (N, 8, 16, W)); h = (W - 1) * rng.integers(0, 2, (N, 8, 4, T, 16)); th = 2016 * rng.integers(0, 2, (N, 8, 16))
    four = np.array([1, 2, W - 17, W - 2])
    for g in (0, 2, 4, 6, 7):
        e = 63 * rng.integers(0, 2, (N, 1)); x[:, g, :, 0] = e; x[:, g, :, W - 1] = 63 - e
        for j in range(4):
            x[:, g, :, int(four[j])] = np.where((j == 0) | (kk % 3 == j - 1), e, 63 - e)
    def zip3(j):
        return np.where(j < 3 * (Z // 3), j % 3, 3)
    a, b = kk < Z, kk >= 16 - Z
    top = np.where(a, zip3(kk), np.where(b, zip3(kk - 16 + Z), 1 + (kk & 1)))
    t2 = np.where(a, 0, np.where(b, 1, 2)); t3 = np.where(a, 2, np.where(b, 0, 1))
    late = np.where(b, 0, 2)
    turn = np.array([[0, 1, 2, 3], [0, 2, 1, 3], [0, 2, 3, 1]])
    def seq(z, j):
        return np.where((j == Z - 1) | (j % 3 == 0), z, np.where(j % 3 == 1, 0, 3 - z))
    def great(zl, zr, at):
        z = np.where(b, seq(zr, kk - 16 + Z), np.where(a, seq(zl, kk), zl))
        return np.where(a | b | (kk == at), four[turn[z]].T, lay(np.zeros((1, 16), np.int64), 0, W - 1)[:, 0])
    for g in (0, 7):
        for i, z in ((0, top), (1, late), (2, t3), (3, t2), (T - 5, t3), (T - 3, late), (T - 2, t2), (T - 1, top)):
            h[:, g, :, i] = lay(z[None, :], 0, W - 1)[:, 0]
        h[:, g, :, 4] = 0; h[:, g, :, T - 4] = W - 1
        for i, s in ((5, great(2, 1, 15 - Z)), (6, great(1, 2, Z)), (T - 7, great(1, 2, 15 - Z)), (T - 6, great(2, 1, Z))):
            h[:, g, :, i] = s
    th[:, ::2, 15] = 2016; th[:, 1::2, 15] = 0; th[:, ::2, 0] = 0; th[:, 1::2, 0] = 2016
    return pack(x, h, th)
def setup_inputs_corners(rng):
    x, h, th = parts(rng); own = 16 * np.arange(T)[:, None] + kk
    th = rng.choice(np.array([0, 1, 31, 600, 700, 2015, 2016]), (N, 8, 16))
    for q in range(N):
        for g in range(8):
            c = (q + g) % 8
            if c == 0: h[q, g] = 0
            if c == 1: h[q, g] = W - 1
            if c == 2: h[q, g] = own
            if c == 3: h[q, g, 0] = own; h[q, g, 1] = W - 1 - own; h[q, g, 2] = 0; h[q, g, 3] = W - 1
            if c == 4: h[q, g] = h[q, g, 0].copy()
            if c == 5: h[q, g] = rng.choice(np.array([Z, 16 * (T - 1) + 16 - Z, 0, W - 1]), (4, T, 16))
            if c == 6: h[q, g, :, ::2] = 0
            if c == 7: h[q, g, :, 1::2] = rng.choice(W - np.array([3, 5, 7, 9, 19, 21]), (4, T // 2, 16)); th[q, g] = rng.choice(np.array([0, 1, 31]), 16)
    return pack(x, h, th)
def setup_inputs_crowd(rng):
    x, h, th = parts(rng)
    x[:, :, 0] = (x[:, :, 0] & 62) | (np.arange(W) & 1); x[..., 2::4] = x[..., 0::4]; x[..., 3::4] = x[..., 1::4]
    p = rng.integers(0, 3, (N, 8, T)); q = (p + rng.integers(1, 3, (N, 8, T))) % 3
    n = np.array([T, T - 1, 0, 1, 31, 32, T // 2, T - 32])[(np.arange(8)[None, :] + np.arange(N)[:, None]) % 8]
    n[N - 1] = np.array([T, T - 1, T, T - 1, T - 1, T - 1, T - 1, T])
    q = np.where(np.argsort(rng.random((N, 8, T)), axis=-1) < n[..., None], q, p)
    at = rng.integers(Z, 17 - Z, (N, 8, T)); at[..., 0] = Z; at[..., T - 1] = 16 - Z
    u = 2 * rng.integers(0, W // 2, (N, 8, T, 16)); v = 2 * rng.integers(0, W // 2, (N, 8, T, 16)) + 1
    h = lay(np.where(kk < at[..., None], p[..., None], q[..., None]), u, v) ^ (2 * rng.integers(0, 2, (N, 8, 4, T, 16)))
    return pack(x, h, th)
def setup_inputs_ties(rng):
    x, h, th = parts(rng); top = rng.integers(1, 4, (N, 8, 1, 1)); top[:, 7] = 1; top[:, 0] = 3
    x = np.minimum((rng.random((N, 8, 16, W)) * (top + 1)).astype(np.int64), top)
    h[:, ::2, :, ::2] = lay(rng.integers(0, 4, (N, 4, T // 2, 16)), rng.integers(0, W, (N, 4, T // 2, 16)), rng.integers(0, W, (N, 4, T // 2, 16)))
    return pack(x, h, rng.integers(0, 21, (N, 8, 16)))
def check_inputs(d):
    bad = []
    for k, lo, hi in (("x", 0, 63), ("hom", 0, W - 1), ("th", 0, 2016)):
        a = np.asarray(d[k]).astype(np.float64)
        if not (np.min(a) >= lo and np.max(a) <= hi): bad.append("range of " + k)
        elif np.any(a != np.floor(a)): bad.append("whole numbers in " + k)
    return bad
def reference(x, hom, th):
    v = x.astype(np.float32).astype(np.int32).reshape(N, 8, 16, W)
    s = np.stack([gentries(a) for a in hom]).astype(np.int64).reshape(N, 8, 4, T, 16)
    t = th.astype(np.int64).reshape(N, 8, 1, 16); A = np.zeros((N, 8), np.int64)
    strand = np.arange(4)[None, None, :, None, None]
    for visit in range(VI):
        p = [np.take_along_axis(v, s[:, :, a].reshape(N, 8, 1, 16 * T), 3) for a in range(4)]
        def dist(a, b):
            return np.add.reduce(np.abs(p[a] - p[b]), axis=2).reshape(N, 8, T, 16).astype(np.int64)
        c = np.stack([dist(0, 1) + dist(2, 3), dist(0, 2) + dist(1, 3), dist(0, 3) + dist(1, 2)])
        L = np.argmin(np.add.reduce(c[..., :Z], axis=-1), axis=0); R = np.argmin(np.add.reduce(c[..., 16 - Z:], axis=-1), axis=0)
        cl = np.take_along_axis(c, L[None, ..., None], 0)[0]; cr = np.take_along_axis(c, R[None, ..., None], 0)[0]
        tot = np.stack([np.add.reduce(cl[..., :m], axis=-1) + np.add.reduce(cr[..., m:], axis=-1) for m in range(Z, 17 - Z)])
        meet = Z + np.argmin(tot, axis=0)
        right = kk >= meet[..., None]
        over = np.where(right, cr, cl) > t + (A & 31)[:, :, None, None]
        mate = strand ^ (np.where(right, R[..., None], L[..., None])[:, :, None] + 1)
        new = ((s * np.take_along_axis(s, mate, 2) >> SH) + s + 37 * kk) & (W - 1)
        s = np.where(over[:, :, None] & (mate < strand), new, s)
        sw = L != R
        s = np.where((sw[..., None] & right)[:, :, None], np.take_along_axis(s, mate, 2), s)
        at = (kk == meet[..., None]).reshape(N, 8, 1, 16 * T)
        v[..., :16 * T] = np.where(at, (v[..., :16 * T] + p[0]) >> 1, v[..., :16 * T])
        A = np.add.reduce(sw.astype(np.int64), axis=-1)
        s = np.stack([np.roll(s[:, :, a], STEP[a], axis=0) for a in range(4)], axis=2)
    return {"yx": v.reshape(N, 128, W).astype(np.float32).astype(BF), "ys": np.stack([gtable(a.reshape(8, -1)) for a in s]).astype(np.float32)}

@@ -1,0 +1,536 @@
+from concourse.bass import DstId, RemoteDMATransfer
+from concourse.mybir import AluOpType as ALU, ActivationFunctionType as AF
+
+NR, VI, TT, WX = 8, 6, 128, 2048
+STEP = (0, 1, 3, 4)
+NCH = 2
+N = TT // NCH
+NB = N // 32
+PC = 512
+OFFK = 12582912.0
+MAGIC = 201326592.0
+H = "float16"
+S_, P_ = "sbuf", "psum"
+
+SCRATCH = {
+    "xs": (S_, [128, WX], "bfloat16"), "p0": (S_, [128, WX], "bfloat16"),
+    "dd": (S_, [128, 3 * WX], "bfloat16"), "ab": (S_, [128, 6 * WX], "bfloat16"),
+    "homi": (S_, [128, 512], "int32"), "thi": (S_, [128, 8], "int32"), "thr": (S_, [128, 8], "float32"),
+    "off": (S_, [128, (VI + 1) * 512], "uint16"), "outb": (S_, [128, VI * 384], "uint16"),
+    "sh": (S_, [128, 2 * 7 * TT], H), "ysf": (S_, [128, 512], "float32"),
+    "ji": (S_, [128, 144], "int32"), "jf": (S_, [128, 144], "float32"), "jg": (S_, [128, 128], "int32"), "jk": (S_, [128, N], "int32"),
+    "pi": (S_, [128, 8], "int32"), "cf": (S_, [128, 24], "float32"),
+    "wb": (S_, [128, 144], "bfloat16"), "wn": (S_, [128, 144], "bfloat16"), "ib": (S_, [128, 256], "bfloat16"), "ih": (S_, [128, 256], H),
+    "zm": (S_, [128, 512], H), "pm": (S_, [128, 512], "bfloat16"),
+    "ka": (S_, [128, 128], "bfloat16"), "kb": (S_, [128, 4 * N], "bfloat16"), "zb": (S_, [128, 3 * N], "bfloat16"),
+    "lci": (S_, [128, 8], "float32"), "lc": (S_, [128, 8], "bfloat16"), "zf": (S_, [128, N], "float32"),
+    "m192": (S_, [128, N], "bfloat16"), "rst": (S_, [128, N], "float32"), "keep": (S_, [128, N], "float32"),
+    "ch": (S_, [128, 384], H), "k0": (S_, [128, 256], "float32"), "m1": (S_, [128, 256], "float32"),
+    "mk": (S_, [128, 256], "int32"), "xi": (S_, [128, 512], "int32"), "df": (S_, [128, 256], "float32"),
+    "dq": (S_, [128, 128], "float32"), "dv": (S_, [128, 128], "float32"), "uu": (S_, [128, 128], "float32"),
+    "rt": (S_, [128, 128], "float32"), "run": (S_, [128, 128], "bfloat16"),
+    "cp": (S_, [128, 256], "float32"), "ov": (S_, [128, 128], "float32"), "fm": (S_, [128, 256], "bfloat16"),
+    "sw": (S_, [128, 128], "bfloat16"), "sg": (S_, [128, 256], "float32"), "cnt": (S_, [128, 8], "float32"),
+    "ai": (S_, [128, 8], "int32"), "lst": (S_, [128, 8], "uint16"),
+    "tq": (S_, [128, 256], H), "a2": (S_, [128, 128], H), "pr": (S_, [128, 256], "float32"),
+    "yy": (S_, [128, 256], "float32"), "bi": (S_, [128, 256], "int32"), "bn": (S_, [128, 256], "int32"),
+    "bh": (S_, [128, 256], H), "ee": (S_, [128, 256], H), "qq": (S_, [128, 256], H),
+    "bu": (S_, [128, 128], "float32"), "bv": (S_, [128, 128], "float32"), "bw": (S_, [128, 128], "bfloat16"),
+    "pd0": (P_, [128, 512], "float32"), "pd1": (P_, [128, 512], "float32"), "pc": (P_, [128, 512], "float32"),
+    "pk": (P_, [128, 512], "float32"), "pl": (P_, [128, 512], "float32"), "r1": (P_, [128, 512], "float32"),
+    "r2": (P_, [128, 512], "float32"), "r3": (P_, [128, 512], "float32"),
+}
+SEMAPHORES = (["cv", "ca", "cp", "cg", "sent", "ld0", "ld1", "ld2", "ld3", "st0", "st1"]
+              + ["a%d_%d_%d" % (v, c, s) for v in range(VI) for c in range(NCH) for s in (1, 2, 3)])
+
+CFG = {"cyc": 1.04, "pe": 0.52, "gath": 1.56, "scat": 3.8, "net": 5500.0, "ov": 55.0, "oa": 70.0, "lam": 2000.0, "theta": 0.2, "ls": 60.0, "lx": 110.0,
+       "relu": (),
+       "actm": ("fm", "k0", "bv"),
+       "pa": 512,
+       "rs": 16,
+       "pri": []}
+_PLAN = {}
+
+
+def routes(T, topo):
+    out = {}
+    for r in range(NR):
+        src = T.cores[r]
+        used, direct, relayed = [], [], []
+        for s in (3, 2, 1):
+            dst = T.cores[(r + STEP[s]) % NR]
+            if topo.may_write(src, dst):
+                direct.append((s, dst))
+            else:
+                cand = [c for c in topo.cores_of(src) if c != src and c not in used and topo.may_write(c, dst)]
+                cand.sort(key=lambda c: (topo.die(c) != topo.die(src), c))
+                used.append(cand[0])
+                relayed.append((s, cand[0]))
+        taken = []
+        for s, dst in direct:
+            free = [e for e in topo.engines(src, dst) if e not in taken][:4]
+            taken += free
+            out[(r, s)] = (dst, None, sum(1 << e for e in free))
+        for j, (s, rel) in enumerate(relayed):
+            free = [e for e in topo.engines(src, rel) if e not in taken]
+            free = free[-8:] if j == 0 else free[-4:]
+            taken += free
+            out[(r, s)] = (rel, rel, sum(1 << e for e in free))
+    return out
+
+
+def bits(m):
+    return bin(m).count("1")
+
+
+def ocol(v, c, s):
+    return s * TT + c * N if v == 0 else v * 512 + c * 4 * N + s * N
+
+
+def schedule(ops):
+    n, pri = len(ops), CFG["pri"]
+    succ = [[] for _ in range(n)]
+    for i, o in enumerate(ops):
+        for d in o["deps"]:
+            succ[d].append(i)
+    pr = [0.0] * n
+    for i in range(n - 1, -1, -1):
+        pr[i] = ops[i]["cost"] + max([pr[j] + 100.0 for j in succ[i]] + [0.0])
+    pr = [pr[i] - CFG["lam"] * ops[i]["grp"] + (pri[ops[i]["typ"]] if 0 <= ops[i]["typ"] < len(pri) else 0.0) for i in range(n)]
+    left = [len(o["deps"]) for o in ops]
+    ready = [0.0] * n
+    free, order, pool = {}, {}, {}
+    for i, o in enumerate(ops):
+        free[o["q"]] = 0.0
+        order.setdefault(o["q"], [])
+        pool.setdefault(o["q"], [])
+        if left[i] == 0:
+            pool[o["q"]].append(i)
+    done, end = 0, 0.0
+    while done < n:
+        best = None
+        for q in pool:
+            if pool[q]:
+                t = max(free[q], min(ready[i] for i in pool[q]))
+                if best is None or t < best[0]:
+                    best = (t, q)
+        t, q = best
+        i = max([j for j in pool[q] if ready[j] <= t + 1.0], key=lambda j: (pr[j], -j))
+        soon = [j for j in pool[q] if pr[j] > pr[i] and ready[j] <= t + CFG["theta"] * ops[i]["hold"]]
+        if soon and q != "N":
+            free[q] = min(ready[j] for j in soon)
+            continue
+        pool[q].remove(i)
+        order[q].append(i)
+        t = max(t, ready[i])
+        fin = t + ops[i]["cost"]
+        ops[i]["t"] = t
+        if q != "N":
+            free[q] = t + ops[i]["hold"]
+        end = max(end, fin)
+        done += 1
+        for j in succ[i]:
+            lat = 0.0 if ops[j]["q"] == q == "P" else (CFG["ls"] if ops[j]["q"] == q else CFG["lx"])
+            ready[j] = max(ready[j], fin + lat)
+            left[j] -= 1
+            if left[j] == 0:
+                pool[ops[j]["q"]].append(j)
+    return order, end
+
+
+def build(g, core, T, topo, rank, rt):
+    ops, lastw, readers, lock = [], {}, {}, {}
+    grp = [0, 100000]
+    V, A, PE = g.vector, g.scalar, g.tensor
+    CYC, GATH, RELU, ACTM, PA, RS = CFG["cyc"], CFG["gath"], CFG["relu"], CFG["actm"], CFG["pa"], CFG["rs"]
+
+    def add(q, fn, cost, r=(), w=(), bank=(), sem=None, hold=None, after=()):
+        i = len(ops)
+        deps = set(after)
+        for t in r:
+            if t in lastw:
+                deps.add(lastw[t])
+        for t in w:
+            if t in lastw:
+                deps.add(lastw[t])
+            deps.update(readers.get(t, ()))
+        for b in bank:
+            users = lock.setdefault(b, [])
+            if users and ops[users[-1]]["q"] != q:
+                lock[(b, "pre")] = list(users)
+                lock[b] = users = []
+            deps.update(lock.get((b, "pre"), ()))
+            users.append(i)
+        for t in r:
+            readers.setdefault(t, []).append(i)
+        for t in w:
+            lastw[t] = i
+            readers[t] = []
+        deps.discard(i)
+        ops.append({"q": q, "fn": fn, "cost": cost, "deps": sorted(deps), "sem": sem, "hold": cost if hold is None else hold,
+                    "grp": grp[0], "typ": i - grp[1]})
+        return i
+
+    def vc(cyc):
+        return CFG["ov"] + max(64.0, cyc) * CYC
+
+    def ts(out, in0, s1, s2, o0, o1, cyc, r, w, bank=()):
+        if o1 is None:
+            return add("V", lambda: V.tensor_scalar(out, in0, s1, None, o0), vc(cyc), r, w, bank)
+        return add("V", lambda: V.tensor_scalar(out, in0, s1, s2, o0, o1), vc(cyc), r, w, bank)
+
+    def tt(out, in0, in1, op, cyc, r, w, bank=()):
+        return add("V", lambda: V.tensor_tensor(out, in0, in1, op), vc(cyc), r, w, bank)
+
+    def cp(out, in_, cyc, r, w, bank=()):
+        return add("V", lambda: V.tensor_copy(out, in_), vc(cyc), r, w, bank)
+
+    def ms(out, val, cyc, w):
+        return add("V", lambda: V.memset(out, val), vc(cyc), (), w)
+
+    def scan(out, d0, d1, o0, o1, r, w):
+        return add("V", lambda: V.tensor_tensor_scan(out, d0, d1, 0.0, o0, o1), vc(N), r, w)
+
+    def turn(out, in_, r, w, bank=()):
+        return add("V", lambda: V.transpose(out, in_), vc(N), r, w, bank)
+
+    def act(out, in_, f, cyc, r, w, bank=(), **kw):
+        return add("A", lambda: A.activation(out, in_, f, **kw), CFG["oa"] + max(64.0, cyc) * CYC, r, w, bank)
+
+    def mm(lst, r, w, bank):
+        def fn():
+            ins = None
+            for (o, l, x, st, sp) in lst:
+                ins = PE.matmul(o, l, x, st, sp)
+            return ins
+        return add("P", fn, 40.0 + sum(max(64, m[2].shape[1]) * CFG["pe"] for m in lst), r, w, bank)
+
+    def lin(bank, terms, r, w):
+        return mm([(o, T.ih[:, 0:128] if sg > 0 else T.ih[:, 128:256], x, bool(a), bool(b)) for (o, sg, x, a, b) in terms], list(r) + ["ih"], w, [bank])
+
+    def dma(q, out, in_, sem, r, w):
+        e = g.sync if q == "S" else g.scalar
+        return add(q, lambda: e.dma_start(out, in_), 2500.0, r, w, sem=(sem, 16), hold=60.0)
+
+    def iota(out, pat, base, mult, cyc, w, small=False):
+        if small:
+            return add("G", lambda: g.iota(out, pat, base, mult, allow_small_or_imprecise_dtypes=True), 130.0 + 2 * cyc, (), w)
+        return add("G", lambda: g.iota(out, pat, base, mult), 130.0 + 2 * cyc, (), w)
+
+    def col(j):
+        return T.cf[:, j:j + 1]
+
+    dma("S", T.homi[:], T.hom[:], "ld0", (), ["homi"])
+    dma("A", T.xs[:, 0:1024], T.x[:, 0:1024], "ld1", (), ["xa"])
+    dma("S", T.xs[:, 1024:2048], T.x[:, 1024:2048], "ld2", (), ["xb"])
+    dma("A", T.thi[:, 0:1], T.th[:], "ld3", (), ["thi"])
+    X = ["xa", "xb"]
+    iota(T.pi[:, 0:1], [[0, 1]], 0, 1, 1, ["pi0"])
+    iota(T.ji[:], [[1, 144]], 0, 0, 144, ["ji"])
+    iota(T.lci[:, 0:2 * NB], [[256, 2], [512, NB]], 16, 0, 8, ["lci"], True)
+    ts(T.pi[:, 1:2], T.pi[:, 0:1], 112, None, ALU.bitwise_and, None, 1, ["pi0"], ["pi1"])
+    ts(T.pi[:, 2:3], T.pi[:, 0:1], 15, None, ALU.bitwise_and, None, 1, ["pi0"], ["pi2"])
+    ts(T.pi[:, 3:4], T.pi[:, 0:1], 16, None, ALU.bitwise_and, None, 1, ["pi0"], ["pi3"])
+    cp(T.cf[:, 0:4], T.pi[:, 0:4], 4, ["pi0", "pi1", "pi2", "pi3"], ["c0"])
+    cP, cG, cK, cH = col(0), col(1), col(2), col(3)
+    cp(T.jf[:], T.ji[:], 144, ["ji"], ["jf"])
+    ts(T.jg[:], T.ji[:, 0:128], 112, None, ALU.bitwise_and, None, 128, ["ji"], ["jg"])
+    ts(T.jk[:], T.ji[:, 0:N], 15, None, ALU.bitwise_and, None, N, ["ji"], ["jk"])
+    ts(T.rst[:], T.jk[:], 15.0, None, ALU.is_equal, None, N, ["jk"], ["rst"])
+    ts(T.keep[:], T.jk[:], 0.0, None, ALU.not_equal, None, N, ["jk"], ["keep"])
+    ts(T.wb[:], T.jf[:], cG, 15.0, ALU.subtract, ALU.is_equal, 144, ["jf", "c0"], ["wb"])
+    if RELU:
+        ts(T.wn[:], T.wb[:], -1.0, None, ALU.mult, None, 72, ["wb"], ["wn"])
+    for buf, nm in ((T.ib, "ib"), (T.ih, "ih")):
+        ts(buf[:, 0:128], T.jf[:, 0:128], cP, 1.0, ALU.is_equal, ALU.mult, 128, ["jf", "c0"], [nm])
+        ts(buf[:, 128:256], T.jf[:, 0:128], cP, -1.0, ALU.is_equal, ALU.mult, 128, ["jf", "c0"], [nm])
+    ms(T.zb[:], 0.0, 96, ["zb"])
+    ms(T.zf[:], 0.0, N, ["zf"])
+    ms(T.m192[:], -192.0, 64, ["m192"])
+    ms(T.ka[:], 2048.0, 64, ["ka"])
+    for j, (lim, op, val) in enumerate(((3.0, ALU.is_lt, 4096.0), (3.0, ALU.is_lt, -4096.0), (13.0, ALU.is_ge, 4096.0), (13.0, ALU.is_ge, -4096.0))):
+        ts(col(4 + j), cK, lim, val, op, ALU.mult, 1, ["c0"], ["c%d" % (4 + j)])
+        ts(T.zm[:, 128 * j:128 * j + 128], T.jg[:], cG, col(4 + j), ALU.is_equal, ALU.mult, 128, ["jg", "c0", "c%d" % (4 + j)], ["zm"])
+    ts(col(8), cK, 3.0, 16.0, ALU.is_ge, ALU.mult, 1, ["c0"], ["c8"])
+    ts(col(9), cK, 12.0, col(8), ALU.is_le, ALU.mult, 1, ["c0", "c8"], ["c9"])
+    ts(col(10), cK, 3.0, -1.0e7, ALU.is_lt, ALU.mult, 1, ["c0"], ["c10"])
+    ts(col(12), col(10), 1.0, None, ALU.add, None, 1, ["c10"], ["c12"])
+    ts(col(15), cK, 592.0, -7.5, ALU.mult, ALU.add, 1, ["c0"], ["c15"])
+    for jh in range(2):
+        ts(col(16 + jh), cH, 16.0 * jh, -1.0, ALU.is_equal, ALU.mult, 1, ["c0"], ["c%d" % (16 + jh)])
+    ts(col(18), cP, 16.0, None, ALU.add, None, 1, ["c0"], ["c18"])
+    ts(col(19), cP, -16.0, None, ALU.add, None, 1, ["c0"], ["c19"])
+    for jh in range(2):
+        for h in range(2):
+            sc = cP if h == jh else col(18 if h > jh else 19)
+            j = 2 * jh + h
+            ts(T.pm[:, 128 * j:128 * j + 128], T.jf[:, 0:128], sc, col(16 + jh), ALU.is_equal, ALU.mult, 128,
+               ["jf", "c0", "c16", "c17", "c18", "c19"], ["pm"])
+    ts(col(20), cK, 16.0, None, ALU.mult, None, 1, ["c0"], ["c20"])
+    ts(T.lc[:, 0:2 * NB], T.lci[:, 0:2 * NB], col(20), None, ALU.add, None, 8, ["lci", "c20"], ["lc"])
+    ts(col(21), cP, 0.0, 6144.0, ALU.is_equal, ALU.mult, 1, ["c0"], ["c21"])
+    ts(col(22), cP, 1.0, None, ALU.is_equal, None, 1, ["c0"], ["c22"])
+    for p in (1, 2):
+        ts(col(23), col(22), float(p), col(21), ALU.mult, ALU.add, 1, ["c21", "c22"], ["c23"])
+        ts(T.kb[:, 2 * (p - 1) * N:2 * p * N], T.zb[:, 0:2 * N], col(23), None, ALU.add, None, N, ["zb", "c23"], ["kb"])
+    cp(T.thr[:, 0:1], T.thi[:, 0:1], 1, ["thi"], ["thr"])
+    for s in range(4):
+        cp(T.off[:, s * TT:(s + 1) * TT], T.homi[:, s * TT:(s + 1) * TT], TT, ["homi"], [("off", 0, c, s) for c in range(NCH)])
+
+    nd = [0]
+    sent = [0]
+    for v in range(VI):
+        grp[1] = len(ops)
+        for c in range(NCH):
+            grp[0] = v * NCH + c
+
+            def sl(buf, k, j=0, m=1):
+                return buf[:, (c * k + j) * N:(c * k + j + m) * N]
+
+            def tk(name):
+                return (name, c)
+
+            def ps(buf, j, m=1):
+                return buf[:, j * N:(j + m) * N]
+
+            def rev(buf, a):
+                return buf[:, a + N - 1:(a - 1 if a else None):-1]
+
+            def st(u, j, m=1):
+                a = ((u % 2) * NCH + c) * 7 * N + j * N
+                return T.sh[:, a:a + m * N]
+            SH = [st(v, 0), st(v, 4), st(v, 5), st(v, 6)]
+            shk, s0k = ("sh", v % 2, c), ("s0", v % 2, c)
+            if v > 0:
+                a = ocol(v, c, 1)
+                cp(st(v, 4, 3), T.off[:, a:a + 3 * N], 1.5 * N, [("off", v, c, s) for s in (1, 2, 3)], [shk])
+            else:
+                grp[1] += 3
+                for s in range(4):
+                    cp(SH[s], T.homi[:, s * TT + c * N:s * TT + (c + 1) * N], N, ["homi"], [shk if s else s0k])
+            c0 = c * 16 * N
+            pieces = list(range(c0, c0 + 16 * N, PC))
+            mm([(T.pc[:, 0:3 * N], T.zb[:, 0:128], T.zb[:, 0:3 * N], True, False)], ["zb"], ["C"], ["pc"])
+
+            def ind(s, a):
+                o = ocol(v, c, s) + (a - c0) // 16
+                return T.xs[:, 0:WX].indirect(T.off[:, o:o + PC // 16])
+            for a in pieces:
+                act(T.p0[:, a:a + PC], ind(0, a), AF.Identity, PC * GATH, X + [("off", v, c, 0)], [("p0", a)])
+            for s in (2, 1, 3):
+                for a in pieces:
+                    o = (s - 1) * WX + a
+                    tt(T.dd[:, o:o + PC], ind(s, a), T.p0[:, a:a + PC], ALU.subtract, PC * GATH, X + [("off", v, c, s), ("p0", a)], [("dd", s, a)])
+                for a in range(c0, c0 + 16 * N, PA):
+                    o = (s - 1) * WX + a
+                    rr, ww = [("dd", s, b) for b in range(a, a + PA, PC)], [("ab", s - 1, b) for b in range(a, a + PA, PC)]
+                    if s in RELU:
+                        ts(T.ab[:, o:o + PA], T.dd[:, o:o + PA], 0.0, 2.0, ALU.max, ALU.mult, PA / 2, rr, ww)
+                    else:
+                        act(T.ab[:, o:o + PA], T.dd[:, o:o + PA], AF.Abs, PA, rr, ww)
+                for p, (s1, s2) in {2: (), 1: ((2, (1, 2)),), 3: ((1, (1, 3)), (0, (2, 3)))}[s]:
+                    for a in pieces:
+                        bk = "pd%d" % (nd[0] % 2)
+                        nd[0] += 1
+                        o1, o2, o = (s1 - 1) * WX + a, (s2 - 1) * WX + a, (3 + p) * WX + a
+                        mm([(T[bk][:, 0:PC], T.ib[:, 0:128], T.dd[:, o1:o1 + PC], True, False),
+                            (T[bk][:, 0:PC], T.ib[:, 128:256], T.dd[:, o2:o2 + PC], False, True)], ["ib", ("dd", s1, a), ("dd", s2, a)], [bk], [bk])
+                        act(T.ab[:, o:o + PC], T[bk][:, 0:PC], AF.Abs, PC, [bk], [("ab", 3 + p, a)], [bk])
+            arrs = [(s - 1, T.dd, T.wn, ["wn"] + [("dd", s, a) for a in pieces]) for s in RELU]
+            arrs += [(ar, T.ab, T.wb, ["wb"] + [("ab", ar, a) for a in pieces]) for ar in (1, 0, 5, 2, 4, 3)]
+            for j, (ar, buf, wm, rr) in enumerate(arrs):
+                p, base = ar % 3, ar * WX + c0
+                for k0 in range(0, 16, RS):
+                    last = j == len(arrs) - 1 and k0 + RS == 16
+                    mm([(ps(T.pc, p), wm[:, 15 - k:143 - k], buf[:, base + k:base + 16 * N:16], False, last and k == 15)
+                        for k in range(k0, k0 + RS)], rr + ([] if last else ["C"]), ["C"] if last else [], ["pc"])
+            cp(sl(T.ch, 3, 0, 3), ps(T.pc, 0, 3), 3 * N, ["C"], [tk("ch")], ["pc"])
+            for e in range(2 if "k0" in ACTM else 1):
+                act(sl(T.k0, 2, e), ps(T.pc, 0), AF.Identity, N, ["C"], [("k0", c, e)], ["pc"], bias=OFFK)
+            mm([(ps(T.pk, 0, 4), T.ka[:], T.kb[:], True, False)], ["ka", "kb"], ["K", "K1", "K2"], ["pk"])
+            lst = []
+            for p in (1, 2):
+                for e in range(2):
+                    o = ps(T.pk, 2 * (p - 1) + e)
+                    lst += [(o, T.zm[:, 256 * e:256 * e + 128], sl(T.ch, 3, p), False, False),
+                            (o, T.zm[:, 256 * e + 128:256 * e + 256], sl(T.ch, 3, 0), False, False),
+                            (o, T.ih[:, 0:128], sl(T.ch, 3, p), False, p == 2 and e == 1)]
+            mm(lst, ["zm", "ih", tk("ch")], ["K"], ["pk"])
+            if "k0" in ACTM:
+                tt(sl(T.m1, 2, 0, 2), ps(T.pk, 0, 2), sl(T.k0, 2, 0, 2), ALU.min, 2 * N, ["K", ("k0", c, 0), ("k0", c, 1)], [("m1", c, 0), ("m1", c, 1)], ["pk"])
+            else:
+                for e in range(2):
+                    tt(sl(T.m1, 2, e), ps(T.pk, e), sl(T.k0, 2, 0), ALU.min, N, ["K", ("k0", c, 0)], [("m1", c, e)], ["pk"])
+            tt(sl(T.mk, 2, 0, 2), ps(T.pk, 2, 2), sl(T.m1, 2, 0, 2), ALU.min, 2 * N, ["K", ("m1", c, 0), ("m1", c, 1)], [tk("mk")], ["pk"])
+            ts(sl(T.xi, 4, 0, 2), sl(T.mk, 2, 0, 2), 2047, None, ALU.bitwise_and, None, 2 * N, [tk("mk")], [tk("xc")])
+            tt(sl(T.df, 2, 0), sl(T.xi, 4, 0), sl(T.xi, 4, 1), ALU.subtract, 2 * N, [tk("xc")], [tk("D")])
+            ts(sl(T.xi, 4, 2, 2), sl(T.mk, 2, 0, 2), 11, 3, ALU.arith_shift_right, ALU.bitwise_and, 2 * N, [tk("mk")], [tk("xp")])
+            tt(sl(T.df, 2, 1), sl(T.xi, 4, 2), sl(T.xi, 4, 3), ALU.subtract, 2 * N, [tk("xp")], [tk("dp")])
+            if "dq" in ACTM:
+                act(sl(T.dq, 1), sl(T.df, 2, 0), AF.Identity, N, [tk("D"), "c9", "c12"], [tk("dq")], bias=col(12), scale=col(9))
+            else:
+                ts(sl(T.dq, 1), sl(T.df, 2, 0), col(9), col(12), ALU.mult, ALU.add, N, [tk("D"), "c9", "c12"], [tk("dq")])
+            turn(sl(T.dv, 1), sl(T.dq, 1), [tk("dq")], [tk("dv")])
+            scan(sl(T.uu, 1), sl(T.dv, 1), T.zf[:], ALU.add, ALU.max, [tk("dv"), "zf"], [tk("uu")])
+            scan(rev(T.rt, c * N), rev(T.rst, 0), rev(T.uu, c * N), ALU.max, ALU.min, [tk("uu"), "rst"], [tk("rt")])
+            scan(sl(T.run, 1), T.keep[:], sl(T.rt, 1), ALU.mult, ALU.add, [tk("rt"), "keep"], [tk("run")])
+            lo = c * 2 * NB
+            mm([(T.pl[:, 0:2 * NB], T.ib[:, 0:128], T.lc[:, 0:2 * NB], True, False)], ["ib", "lc"], ["L"], ["pl"])
+            mm([(T.pl[:, jh * NB:(jh + 1) * NB], T.pm[:, 128 * (2 * jh + h):128 * (2 * jh + h + 1)],
+                 T.run[:, c * N + 16 * h + 15:(c + 1) * N:32], False, jh == 1 and h == 1) for jh in range(2) for h in range(2)],
+               ["pm", tk("run")], ["L"], ["pl"])
+            cp(T.lst[:, lo:lo + 2 * NB], T.pl[:, 0:2 * NB], 8, ["L"], [tk("lst")], ["pl"])
+            turn(ps(T.pk, 0), sl(T.rt, 1), [tk("rt")], ["K"], ["pk"])
+            tt(ps(T.pk, 2), ps(T.pk, 0), sl(T.df, 2, 1), ALU.mult, N, ["K", tk("dp")], ["K2"], ["pk"])
+            tt(sl(T.cp, 2, 1), sl(T.xi, 4, 2), ps(T.pk, 2), ALU.subtract, N, ["K2", tk("xp")], [tk("P")], ["pk"])
+            tt(ps(T.pk, 1), ps(T.pk, 0), sl(T.df, 2, 0), ALU.mult, N, ["K", tk("D")], ["K1"], ["pk"])
+            tt(sl(T.cp, 2, 0), sl(T.xi, 4, 0), ps(T.pk, 1), ALU.subtract, N, ["K1", tk("xc")], [tk("cp")], ["pk"])
+            ts(sl(T.sw, 1), ps(T.pk, 2), 0.0, None, ALU.not_equal, None, N, ["K2"], [tk("sw")], ["pk"])
+            if "fm" in ACTM:
+                act(sl(T.fm, 2, 0), sl(T.cp, 2, 1), AF.Relu, N, [tk("P")], [tk("f0")], bias=1.0, scale=-1.0)
+                act(sl(T.fm, 2, 1), sl(T.cp, 2, 1), AF.Relu, N, [tk("P")], [tk("f2")], bias=-1.0)
+            else:
+                ts(sl(T.fm, 2, 0), sl(T.cp, 2, 1), 0.0, None, ALU.is_equal, None, N, [tk("P")], [tk("f0")])
+                ts(sl(T.fm, 2, 1), sl(T.cp, 2, 1), 2.0, None, ALU.is_equal, None, N, [tk("P")], [tk("f2")])
+            ts(sl(T.ov, 1), sl(T.cp, 2, 0), T.thr[:, 0:1], 0.0625, ALU.is_gt, ALU.mult, N, [tk("cp"), "thr"], [tk("ov")])
+            F = [tk("f0"), tk("f2")]
+            if v < VI - 1:
+                act(sl(T.sg, 2, 0), sl(T.df, 2, 1), AF.Sign, N, [tk("dp")], [tk("sg0")])
+                act(sl(T.sg, 2, 1), sl(T.sg, 2, 0), AF.Abs, N, [tk("sg0")], [tk("sg1"), tk("cnt")], accum_out=T.cnt[:, c:c + 1])
+            XC = X if NCH == 1 else [X[c]]
+            act(sl(T.bu, 1), T.p0[:, c0:c0 + 16 * N].indirect(T.lst[:, lo:lo + 2 * NB]), AF.Identity, N * GATH,
+                [tk("lst")] + [("p0", a) for a in pieces], [tk("bu")], bias=191.75, scale=0.5)
+            if "bv" in ACTM or ("bv0" in ACTM and c == 0):
+                act(sl(T.bv, 1), T.xs[:, c0:c0 + 16 * N].indirect(T.lst[:, lo:lo + 2 * NB]), AF.Identity, N * GATH, [tk("lst")] + XC, [tk("bv")], scale=0.5)
+            else:
+                ts(sl(T.bv, 1), T.xs[:, c0:c0 + 16 * N].indirect(T.lst[:, lo:lo + 2 * NB]), 0.5, None, ALU.mult, None, N * GATH, [tk("lst")] + XC, [tk("bv")])
+            tt(sl(T.bw, 1), sl(T.bu, 1), sl(T.bv, 1), ALU.add, 2 * N, [tk("bu"), tk("bv")], [tk("bw")])
+            t0, t1, e0, e1, q0, q2 = sl(T.tq, 2, 0), sl(T.tq, 2, 1), sl(T.ee, 2, 0), sl(T.ee, 2, 1), sl(T.qq, 2, 0), sl(T.qq, 2, 1)
+            a2, b1, b2 = st(v, 1), st(v, 2), st(v, 3)
+            a2k, bhk = ("a2", v % 2, c), ("bh", v % 2, c)
+            lin("r1", [(ps(T.r1, 0), 1, SH[2], 1, 0), (ps(T.r1, 0), -1, SH[1], 0, 1), (ps(T.r1, 1), 1, SH[2], 1, 0), (ps(T.r1, 1), -1, SH[3], 0, 1)], [shk], ["R1"])
+            tt(sl(T.tq, 2, 0, 2), ps(T.r1, 0, 2), sl(T.fm, 2, 0, 2), ALU.mult, 2 * N, ["R1"] + F, [tk("tq")], ["r1"])
+            lin("r2", [(ps(T.r2, 0, 2), 1, st(v, 5, 2), 1, 0)], [shk], ["R2"])
+            lin("r2", [(ps(T.r2, 0), -1, t0, 0, 0), (ps(T.r2, 0), -1, t1, 0, 0), (ps(T.r2, 1), 1, t1, 0, 1)], [tk("tq")], ["R2"])
+            tt(a2, t0, SH[1], ALU.add, 2 * N, [shk, tk("tq")], [a2k])
+            tt(sl(T.pr, 2, 0, 2), ps(T.r2, 0, 2), st(v, 0, 2), ALU.mult, 2 * N, ["R2", s0k, a2k], [tk("pr")], ["r2"])
+            ts(ps(T.r1, 0, 2), sl(T.pr, 2, 0, 2), col(15), MAGIC, ALU.add, ALU.add, 2 * N, [tk("pr"), "c15"], ["R1"], ["r1"])
+            for e in range(2):
+                tt(sl(T.yy, 2, e), ps(T.r1, e), sl(T.ov, 1), ALU.mult, N, ["R1", tk("ov")], [("yy", c, e)], ["r1"])
+            tt(sl(T.bi, 2, 0, 2), ps(T.r2, 0, 2), sl(T.yy, 2, 0, 2), ALU.add, 2 * N, ["R2", ("yy", c, 0), ("yy", c, 1)], [tk("bi")], ["r2"])
+            ts(sl(T.bn, 2, 0, 2), sl(T.bi, 2, 0, 2), 2047, None, ALU.bitwise_and, None, 2 * N, [tk("bi")], [tk("bn")])
+            cp(st(v, 2, 2), sl(T.bn, 2, 0, 2), 2 * N, [tk("bn")], [bhk])
+            lin("r2", [(ps(T.r2, 0, 2), -1, st(v, 0, 2), 1, 0)], [s0k, a2k], ["R2"])
+            lin("r2", [(ps(T.r2, 0, 2), 1, st(v, 2, 2), 0, 1)], [bhk], ["R2"])
+            for e in range(2):
+                tt(sl(T.ee, 2, e), ps(T.r2, e), sl(T.sw, 1), ALU.mult, N, ["R2", tk("sw")], [("ee", c, e)], ["r2"])
+            E = [("ee", c, 0), ("ee", c, 1)]
+            lin("r1", [(ps(T.r1, 0, 2), 1, st(v, 2, 2), 1, 0), (ps(T.r1, 0), -1, a2, 0, 0), (ps(T.r1, 1), 1, b1, 0, 0),
+                       (ps(T.r1, 1), -1, b2, 0, 0), (ps(T.r1, 1), -1, b2, 0, 0)], [a2k, bhk], ["R1"])
+            lin("r1", [(ps(T.r1, 0), -1, e0, 0, 0), (ps(T.r1, 0), -1, e1, 0, 0), (ps(T.r1, 1), -1, e0, 0, 0), (ps(T.r1, 1), 1, e1, 0, 1)], E, ["R1"])
+            tt(sl(T.qq, 2, 0, 2), ps(T.r1, 0, 2), sl(T.fm, 2, 0, 2), ALU.mult, 2 * N, ["R1"] + F, [tk("qq")], ["r1"])
+            lin("r3", [(ps(T.r3, 0, 4), 1, st(v, 0, 4), 1, 0)], [s0k, a2k, bhk], ["R3"])
+            lin("r3", [(ps(T.r3, 0, 2), 1, sl(T.ee, 2, 0, 2), 0, 0), (ps(T.r3, 2, 2), -1, sl(T.ee, 2, 0, 2), 0, 0)], E, ["R3"])
+            lin("r3", [(ps(T.r3, 1), 1, q0, 0, 0), (ps(T.r3, 2), -1, q0, 0, 0), (ps(T.r3, 2), -1, q2, 0, 0), (ps(T.r3, 3), 1, q2, 0, 1)], [tk("qq")], ["R3"])
+            ob = v * 384 + c * 3 * N
+            cp(T.outb[:, ob:ob + 3 * N], ps(T.r3, 1, 3), 3 * N, ["R3"], [("outb", v, c)], ["r3"])
+            if v < VI - 1:
+                a = ocol(v + 1, c, 0)
+                cp(T.off[:, a:a + N], ps(T.r3, 0), N, ["R3"], [("off", v + 1, c, 0)], ["r3"])
+                cp(st(v + 1, 0), T.off[:, a:a + N], N / 2, [("off", v + 1, c, 0)], [("s0", (v + 1) % 2, c)])
+            else:
+                cp(T.ysf[:, c * N:(c + 1) * N], ps(T.r3, 0), N, ["R3"], [("ys", c, 0)], ["r3"])
+            trs = []
+            for s in (1, 2, 3):
+                hop, rel, mask = rt[(rank, s)]
+                rid, pid = topo.addr(hop, core)
+                a = ocol(v + 1, c, s)
+                trs.append(RemoteDMATransfer(dst_ids=[DstId(rid=rid, pnc=pid)], dma_engine_mask=mask, remote_sem=T.sem["a%d_%d_%d" % (v, c, s)],
+                                             src=T.outb[:, ob + (s - 1) * N:ob + s * N], dst=T.off[:, a:a + N]))
+                sent[0] += bits(mask)
+            snd = add("G", lambda trs=trs: g.remote_dma_fused(trs, local_sem=T.sem.sent), 1000.0, [("outb", v, c)], (), sem=("", 0))
+            for s in (1, 2, 3):
+                r0 = (rank - STEP[s]) % NR
+                hop, rel, mask = rt[(r0, s)]
+                cntv = bits(mask) if rel is None else bits(topo.mask(rel, core))
+                add("N", None, CFG["net"], (), [("off", v + 1, c, s)], sem=("a%d_%d_%d" % (v, c, s), cntv), after=[snd])
+            if v == VI - 1:
+                for s in (1, 2, 3):
+                    a = ocol(VI, c, s)
+                    cp(T.ysf[:, s * TT + c * N:s * TT + (c + 1) * N], T.off[:, a:a + N], N, [("off", VI, c, s)], [("ys", c, s)])
+        for c in range(NCH):
+            tt(T.xs[:, c * 16 * N:(c + 1) * 16 * N].indirect(T.lst[:, c * 2 * NB:(c + 1) * 2 * NB]), T.bw[:, c * N:(c + 1) * N], T.m192[:], ALU.add,
+               N * CFG["scat"], [("lst", c), ("bw", c), "m192"], X if NCH == 1 else [X[c]])
+        if v < VI - 1:
+            CN = [("cnt", c) for c in range(NCH)]
+            if NCH == 1:
+                cp(T.ai[:, 0:1], T.cnt[:, 0:1], 1, CN, ["ai0"])
+            else:
+                tt(T.ai[:, 0:1], T.cnt[:, 0:1], T.cnt[:, 1:2], ALU.add, 1, CN, ["ai0"])
+            ts(T.ai[:, 1:2], T.ai[:, 0:1], 31, None, ALU.bitwise_and, None, 1, ["ai0"], ["ai1"])
+            tt(T.thr[:, 0:1], T.ai[:, 1:2], T.thi[:, 0:1], ALU.add, 1, ["ai1", "thi"], ["thr"])
+    dma("A", T.yx[:], T.xs[:], "st0", X, ())
+    dma("S", T.ys[:], T.ysf[:], "st1", [("ys", c, s) for c in range(NCH) for s in range(4)], ())
+    return ops, sent[0]
+
+
+def emit(g, T, ops, order, sent):
+    queue = {"V": g.vector, "A": g.scalar, "P": g.tensor, "G": g, "S": g.sync}
+    csem = {"V": "cv", "A": "ca", "P": "cp", "G": "cg"}
+    mark, total = {}, {}
+    for q in order:
+        k = 0
+        for i in order[q]:
+            if ops[i]["sem"] is None:
+                k += 1
+                mark[i] = (csem[q], k)
+            else:
+                mark[i] = ops[i]["sem"]
+        if k:
+            total[csem[q]] = k
+    for q in queue:
+        seen = {}
+        for i in order.get(q, ()):
+            need = {}
+            for d in ops[i]["deps"]:
+                if q == "P" and ops[d]["q"] == "P":
+                    continue
+                s, val = mark[d]
+                need[s] = max(need.get(s, 0), val)
+            for s in need:
+                if need[s] > seen.get(s, 0):
+                    queue[q].wait_ge(T.sem[s], need[s])
+                    seen[s] = need[s]
+            ins = ops[i]["fn"]()
+            s, val = mark[i]
+            if s:
+                ins.then_inc(T.sem[s], 1 if ops[i]["sem"] is None else val)
+    for s in total:
+        g.wait_ge(T.sem[s], total[s])
+    g.wait_ge(T.sem.sent, sent)
+    g.wait_ge(T.sem.st0, 16)
+    g.wait_ge(T.sem.st1, 16)
+
+
+def rank_program(g, core, T, topo):
+    rt = routes(T, topo)
+    rank = T.rank_of(core)
+    if rank is not None:
+        ops, sent = build(g, core, T, topo, rank, rt)
+        if "order" not in _PLAN:
+            _PLAN["order"], _PLAN["end"] = schedule(ops)
+            _PLAN["ops"] = ops
+        emit(g, T, ops, _PLAN["order"], sent)
+        return
+    for (r, s), (hop, rel, mask) in rt.items():
+        if rel == core:
+            dst = T.cores[(r + STEP[s]) % NR]
+            rid, pid = topo.addr(dst, core)
+            m2 = topo.mask(core, dst)
+            for v in range(VI):
+                for c in range(NCH):
+                    a = ocol(v + 1, c, s)
+                    sem = T.sem["a%d_%d_%d" % (v, c, s)]
+                    g.wait_ge(sem, bits(mask))
+                    g.remote_dma(T.off[:, a:a + N], T.off[:, a:a + N], sem, T.sem.sent, pid, rid, m2)
+            g.wait_ge(T.sem.sent, bits(m2) * VI * NCH)

@@ -3,52 +3,48 @@ from concourse.mybir import AluOpType as ALU, ActivationFunctionType as AF
 
 NR, VI, TT, WX = 8, 6, 128, 2048
 STEP = (0, 1, 3, 4)
-NCH = 2
-N = TT // NCH
-NB = N // 32
-PC = 512
+N = 64
+LK = 16 * N
+BLK = 7 * N
 OFFK = 12582912.0
-MAGIC = 201326592.0
-H = "float16"
+M2048 = 25769803776.0
+M16 = 201326592.0
+H, B, F, I = "float16", "bfloat16", "float32", "int32"
 S_, P_ = "sbuf", "psum"
 
+OWN = {"sh": (4, H), "wt": (6, H), "ch": (3, H), "m1": (2, F), "mk": (2, I), "tk": (2, I), "dt": (1, F), "dq": (1, F), "dv": (1, F),
+       "uu": (1, F), "rt": (1, F), "run": (1, B), "tf": (1, I), "xf": (1, I), "fm": (2, H), "ov": (1, H), "junk": (1, F), "tq": (2, H),
+       "ao": (2, F), "pr": (2, F), "zi": (2, I), "bn": (2, I), "dd": (2, H), "ee": (2, H), "qq": (2, H), "bu": (1, F), "bv": (1, F),
+       "bw": (1, B), "bb": (2, B), "wd": (7, H), "ga": (64, B), "ab": (96, B)}
 SCRATCH = {
-    "xs": (S_, [128, WX], "bfloat16"), "p0": (S_, [128, WX], "bfloat16"),
-    "dd": (S_, [128, 3 * WX], "bfloat16"), "ab": (S_, [128, 6 * WX], "bfloat16"),
-    "homi": (S_, [128, 512], "int32"), "thi": (S_, [128, 8], "int32"), "thr": (S_, [128, 8], "float32"),
-    "off": (S_, [128, (VI + 1) * 512], "uint16"), "outb": (S_, [128, VI * 384], "uint16"),
-    "sh": (S_, [128, 2 * 7 * TT], H), "ysf": (S_, [128, 512], "float32"),
-    "ji": (S_, [128, 144], "int32"), "jf": (S_, [128, 144], "float32"), "jg": (S_, [128, 128], "int32"), "jk": (S_, [128, N], "int32"),
-    "pi": (S_, [128, 8], "int32"), "cf": (S_, [128, 24], "float32"),
-    "wb": (S_, [128, 144], "bfloat16"), "wn": (S_, [128, 144], "bfloat16"), "ib": (S_, [128, 256], "bfloat16"), "ih": (S_, [128, 256], H),
-    "zm": (S_, [128, 512], H), "pm": (S_, [128, 512], "bfloat16"),
-    "ka": (S_, [128, 128], "bfloat16"), "kb": (S_, [128, 4 * N], "bfloat16"), "zb": (S_, [128, 3 * N], "bfloat16"),
-    "lci": (S_, [128, 8], "float32"), "lc": (S_, [128, 8], "bfloat16"), "zf": (S_, [128, N], "float32"),
-    "m192": (S_, [128, N], "bfloat16"), "rst": (S_, [128, N], "float32"), "keep": (S_, [128, N], "float32"),
-    "ch": (S_, [128, 384], H), "k0": (S_, [128, 256], "float32"), "m1": (S_, [128, 256], "float32"),
-    "mk": (S_, [128, 256], "int32"), "xi": (S_, [128, 512], "int32"), "df": (S_, [128, 256], "float32"),
-    "dq": (S_, [128, 128], "float32"), "dv": (S_, [128, 128], "float32"), "uu": (S_, [128, 128], "float32"),
-    "rt": (S_, [128, 128], "float32"), "run": (S_, [128, 128], "bfloat16"),
-    "cp": (S_, [128, 256], "float32"), "ov": (S_, [128, 128], "float32"), "fm": (S_, [128, 256], "bfloat16"),
-    "sw": (S_, [128, 128], "bfloat16"), "sg": (S_, [128, 256], "float32"), "cnt": (S_, [128, 8], "float32"),
-    "ai": (S_, [128, 8], "int32"), "lst": (S_, [128, 8], "uint16"),
-    "tq": (S_, [128, 256], H), "a2": (S_, [128, 128], H), "pr": (S_, [128, 256], "float32"),
-    "yy": (S_, [128, 256], "float32"), "bi": (S_, [128, 256], "int32"), "bn": (S_, [128, 256], "int32"),
-    "bh": (S_, [128, 256], H), "ee": (S_, [128, 256], H), "qq": (S_, [128, 256], H),
-    "bu": (S_, [128, 128], "float32"), "bv": (S_, [128, 128], "float32"), "bw": (S_, [128, 128], "bfloat16"),
-    "pd0": (P_, [128, 512], "float32"), "pd1": (P_, [128, 512], "float32"), "pc": (P_, [128, 512], "float32"),
-    "pk": (P_, [128, 512], "float32"), "pl": (P_, [128, 512], "float32"), "r1": (P_, [128, 512], "float32"),
-    "r2": (P_, [128, 512], "float32"), "r3": (P_, [128, 512], "float32"),
+    "xs": (S_, [128, WX], B), "homi": (S_, [128, 512], I), "thi": (S_, [128, 8], I), "thf": (S_, [128, 8], F),
+    "off": (S_, [128, (VI + 1) * 2 * BLK], "uint16"), "ysf": (S_, [128, 512], F), "pi": (S_, [128, 8], I), "cf": (S_, [128, 24], F),
+    "dj": (S_, [128, 128], B), "jg": (S_, [128, 128], B), "j8": (S_, [128, 32], B), "jb": (S_, [128, N], B),
+    "wm": (S_, [128, 384], B), "em": (S_, [128, N], H), "lci": (S_, [128, 8], F), "lc": (S_, [128, 8], B),
+    "ib": (S_, [128, 256], B), "ih": (S_, [128, 256], H), "i16": (S_, [128, 256], H), "dk": (S_, [128, 128], H),
+    "pm": (S_, [128, 512], B), "zm": (S_, [128, 512], H), "jw": (S_, [128, 144], B), "wb": (S_, [128, 432], B), "gm": (S_, [128, 64], B), "sel": (S_, [128, 128], B),
+    "ka": (S_, [128, 128], B), "kb": (S_, [128, 256], B), "zb": (S_, [128, 384], B), "m192": (S_, [128, N], B),
+    "one": (S_, [128, N], F), "kp3": (S_, [128, N], F), "keep": (S_, [128, N], F), "cnt": (S_, [128, 8], F), "lst": (S_, [128, 8], "uint16"),
 }
-SEMAPHORES = (["cv", "ca", "cp", "cg", "sent", "ld0", "ld1", "ld2", "ld3", "st0", "st1"]
-              + ["a%d_%d_%d" % (v, c, s) for v in range(VI) for c in range(NCH) for s in (1, 2, 3)])
+SCRATCH.update({b: (P_, [128, 512], F) for b in ("pd0", "pd1", "pc", "pk", "pl", "r1", "r2", "r3")})
+SCRATCH.update({nm + str(c): (S_, [128, OWN[nm][0] * N], OWN[nm][1]) for nm in OWN for c in range(2)})
+SEMAPHORES = (["cv", "ca", "cp", "cg", "sent", "lx0", "lx1", "lh0", "lh1", "lt", "st"]
+              + ["a%d_%d_%d" % (v, c, s) for v in range(VI) for c in range(2) for s in (1, 2, 3)] + ["d%d" % j for j in range(24)])
 
-CFG = {"cyc": 1.04, "pe": 0.52, "gath": 1.56, "scat": 3.8, "net": 5500.0, "ov": 55.0, "oa": 70.0, "lam": 2000.0, "theta": 0.2, "ls": 60.0, "lx": 110.0,
-       "relu": (),
-       "actm": ("fm", "k0", "bv"),
-       "pa": 512,
-       "rs": 16,
-       "pri": []}
+CFG = {"cyc": 0.9, "pe": 0.5, "gath": 1.56, "scat": 3.8, "net": (0.0, 4800.0, 3600.0, 5600.0), "ov": 50.0, "oa": 65.0, "ls": 140.0, "lx": 210.0,
+       "lam": 4000.0, "delta": 2000.0, "theta": 0.2, "tol": 800.0, "passes": 400, "seeds": (1,), "span": 6, "swaps": 11000, "tol3": 300.0,
+       "cases": ({"cyc": 1.2, "gath": 2.0, "ls": 180.0, "lx": 270.0},
+                 {"cyc": 0.87, "gath": 1.2, "ls": 110.0, "lx": 220.0, "net": (0.0, 5800.0, 4600.0, 6600.0)}),
+       "dma": (), "pd": (512, 512), "dlat": 4000.0,
+       "once": 5000.0, "wait1": 15000.0,
+       "pv": ((512, 512), (512, 512), (512, 512)),
+       "pa": (256, 768),
+       "pb": 512,
+       "rs": 4,
+       "role": (2, 1, 3),
+       "pairs": (((1, 2), (2, 3), (1, 3)), ((1, 2), (2, 3), (1, 3))),
+       "relu": ((1, 3),),
+       "plain": (), "mov": (), "dei": (), "dqa": (), "bwv": (1,)}
 _PLAN = {}
 
 
@@ -56,26 +52,24 @@ def routes(T, topo):
     out = {}
     for r in range(NR):
         src = T.cores[r]
-        used, direct, relayed = [], [], []
-        for s in (3, 2, 1):
+        used, hops = [], []
+        for s in CFG["role"]:
             dst = T.cores[(r + STEP[s]) % NR]
             if topo.may_write(src, dst):
-                direct.append((s, dst))
+                hops.append((s, dst, None))
             else:
                 cand = [c for c in topo.cores_of(src) if c != src and c not in used and topo.may_write(c, dst)]
                 cand.sort(key=lambda c: (topo.die(c) != topo.die(src), c))
                 used.append(cand[0])
-                relayed.append((s, cand[0]))
+                hops.append((s, cand[0], cand[0]))
         taken = []
-        for s, dst in direct:
-            free = [e for e in topo.engines(src, dst) if e not in taken][:4]
-            taken += free
-            out[(r, s)] = (dst, None, sum(1 << e for e in free))
-        for j, (s, rel) in enumerate(relayed):
-            free = [e for e in topo.engines(src, rel) if e not in taken]
-            free = free[-8:] if j == 0 else free[-4:]
-            taken += free
-            out[(r, s)] = (rel, rel, sum(1 << e for e in free))
+        for s, hop, rel in hops:
+            free = [e for e in topo.engines(src, hop) if e not in taken]
+            if len(taken) < 16 and len(free) >= 8:
+                taken += free[:8]
+                out[(r, s)] = (hop, rel, sum(1 << e for e in free[:8]), 0)
+            else:
+                out[(r, s)] = (hop, rel, topo.mask(src, hop), 1)
     return out
 
 
@@ -84,75 +78,194 @@ def bits(m):
 
 
 def ocol(v, c, s):
-    return s * TT + c * N if v == 0 else v * 512 + c * 4 * N + s * N
+    return (v * 2 + c) * BLK + (s - 1 if s else 3) * N
 
 
-def schedule(ops):
-    n, pri = len(ops), CFG["pri"]
+def schedule(cases, start):
+    ops = cases[0][0]
+    n = len(ops)
+    pre = [[(i, ops[i]["hold"] if ops[i]["q"] == o["q"] == "P" else ops[i]["cost"] + (CFG["ls"] if ops[i]["q"] == o["q"] else CFG["lx"]))
+            for i in o["deps"]] for o in ops]
     succ = [[] for _ in range(n)]
-    for i, o in enumerate(ops):
-        for d in o["deps"]:
-            succ[d].append(i)
-    pr = [0.0] * n
+    for j in range(n):
+        for i, l in pre[j]:
+            succ[i].append((j, l))
+    tail = [0.0] * n
     for i in range(n - 1, -1, -1):
-        pr[i] = ops[i]["cost"] + max([pr[j] + 100.0 for j in succ[i]] + [0.0])
-    pr = [pr[i] - CFG["lam"] * ops[i]["grp"] + (pri[ops[i]["typ"]] if 0 <= ops[i]["typ"] < len(pri) else 0.0) for i in range(n)]
-    left = [len(o["deps"]) for o in ops]
-    ready = [0.0] * n
-    free, order, pool = {}, {}, {}
+        tail[i] = max([l + tail[j] for j, l in succ[i]] + [ops[i]["cost"]])
+    first = {}
     for i, o in enumerate(ops):
-        free[o["q"]] = 0.0
-        order.setdefault(o["q"], [])
-        pool.setdefault(o["q"], [])
-        if left[i] == 0:
-            pool[o["q"]].append(i)
-    done, end = 0, 0.0
-    while done < n:
-        best = None
-        for q in pool:
-            if pool[q]:
-                t = max(free[q], min(ready[i] for i in pool[q]))
-                if best is None or t < best[0]:
-                    best = (t, q)
-        t, q = best
-        i = max([j for j in pool[q] if ready[j] <= t + 1.0], key=lambda j: (pr[j], -j))
-        soon = [j for j in pool[q] if pr[j] > pr[i] and ready[j] <= t + CFG["theta"] * ops[i]["hold"]]
-        if soon and q != "N":
-            free[q] = min(ready[j] for j in soon)
+        first.setdefault(o["blk"], i)
+    nt = first[6] - first[4]
+    q_of, hold, cost, blk = [o["q"] for o in ops], [o["hold"] for o in ops], [o["cost"] for o in ops], [o["blk"] for o in ops]
+    place = [(-1 if blk[i] < 0 else min(i - first[blk[i] // 2 * 2], nt - 1)) for i in range(n)]
+    base = [tail[i] - CFG["lam"] * (max(blk[i], 0) // 2) - CFG["delta"] * (max(blk[i], 0) % 2) - CFG["wait1"] * (blk[i] == 1) for i in range(n)]
+    seed = [start]
+
+    def rnd(k):
+        seed[0] = (seed[0] * 1103515245 + 12345) % 2147483648
+        return (seed[0] >> 8) % k
+
+    def listed(off, m):
+        pr = [base[i] + (off[place[i]] if place[i] >= 0 else 0.0) for i in range(m)]
+        left = [len(pre[i]) for i in range(m)]
+        ready, at, free, pool = [0.0] * m, [0.0] * m, {}, {}
+        for i in range(m):
+            free[q_of[i]] = 0.0
+            pool.setdefault(q_of[i], [])
+            if left[i] == 0:
+                pool[q_of[i]].append(i)
+        done, end = 0, 0.0
+        while done < m:
+            t, q = 1e18, None
+            for u in pool:
+                if pool[u]:
+                    w = max(free[u], min([ready[i] for i in pool[u]]))
+                    if w < t:
+                        t, q = w, u
+            p = pool[q]
+            i = max([j for j in p if ready[j] <= t + 1.0], key=lambda j: pr[j])
+            if q != "N":
+                soon = [ready[j] for j in p if pr[j] > pr[i] and ready[j] <= t + CFG["theta"] * hold[i]]
+                if soon:
+                    free[q] = min(soon)
+                    continue
+                free[q] = t + hold[i]
+            p.remove(i)
+            at[i] = t
+            end = max(end, t + cost[i])
+            done += 1
+            for j, l in succ[i]:
+                if j < m:
+                    ready[j] = max(ready[j], t + l)
+                    left[j] -= 1
+                    if left[j] == 0:
+                        pool[q_of[j]].append(j)
+        return at, end
+    m = first[CFG["span"]]
+    off = [0.0] * nt
+    end = listed(off, m)[1]
+    best = (off, end)
+    for it in range(CFG["passes"]):
+        b = list(off)
+        a, w = rnd(nt), (1, 1, 2, 4, 8, 16)[rnd(6)]
+        d = (-1, 1)[rnd(2)] * (150, 400, 1000, 2500, 6000)[rnd(5)]
+        for u in range(a, min(nt, a + w)):
+            b[u] += d
+        e = listed(b, m)[1]
+        if e <= end + CFG["tol"] * (1 - it / CFG["passes"]) * rnd(100) / 100.0:
+            off, end = b, e
+            if end < best[1]:
+                best = (off, end)
+    at0, end0 = listed(best[0], n)
+
+    sends = [at0[i] for i in range(first[0], n) if q_of[i] == "G" and not ops[i]["sem"][0]]
+    per = sends[6] - sends[4]
+    slot, shift, key = [0] * n, [0.0] * n, [at0[i] - 2 * per for i in range(first[4], first[6])]
+    for i in range(n):
+        v = blk[i] // 2
+        if 1 < v < VI - 1:
+            slot[i], shift[i] = i - first[2 * v], v * per
             continue
-        pool[q].remove(i)
-        order[q].append(i)
-        t = max(t, ready[i])
-        fin = t + ops[i]["cost"]
-        ops[i]["t"] = t
-        if q != "N":
-            free[q] = t + ops[i]["hold"]
-        end = max(end, fin)
-        done += 1
-        for j in succ[i]:
-            lat = 0.0 if ops[j]["q"] == q == "P" else (CFG["ls"] if ops[j]["q"] == q else CFG["lx"])
-            ready[j] = max(ready[j], fin + lat)
-            left[j] -= 1
-            if left[j] == 0:
-                pool[ops[j]["q"]].append(j)
-    return order, end
+        slot[i] = len(key)
+        if v < 2:
+            key.append(at0[i] if ops[i]["sem"] is None or v >= 0 else i - 1e3)
+            continue
+        if i == first[blk[i]]:
+            like = first[4 + blk[i] % 2]
+        same = [u for u in range(like, min(like + 12, first[5 + blk[i] % 2])) if q_of[u] == q_of[i] and cost[u] == cost[i]]
+        if same:
+            key.append(max([key[same[0] - first[4]] + v * per] + [key[slot[d]] + shift[d] + 0.01 for d, l in pre[i]]))
+            like = same[0] + 1
+        else:
+            key.append(max([0.0] + [key[slot[d]] + shift[d] + l for d, l in pre[i]]))
+    byq = {}
+    for i in range(n):
+        if q_of[i] != "N":
+            byq.setdefault(q_of[i], []).append(i)
+
+    pres = [[[(i, a[i]["hold"] if q_of[i] == q_of[j] == "P" else a[i]["cost"] + (ls if q_of[i] == q_of[j] else lx)) for i in ops[j]["deps"]]
+             for j in range(n)] for a, ls, lx in cases]
+    holds, costs = [[o["hold"] for o in a] for a, ls, lx in cases], [[o["cost"] for o in a] for a, ls, lx in cases]
+    ends = [i for i in range(n) if not succ[i]]
+
+    def ordered(key, pick):
+        nxt, prv, left = [-1] * n, [-1] * n, [len(p) for p in pre]
+        for q in byq:
+            o = sorted(byq[q], key=lambda i: key[slot[i]] + shift[i])
+            for a, b in zip(o, o[1:]):
+                nxt[a], prv[b] = b, a
+                left[b] += 1
+        seq = [i for i in range(n) if left[i] == 0]
+        for i in seq:
+            for j, l in succ[i]:
+                left[j] -= 1
+                if left[j] == 0:
+                    seq.append(j)
+            j = nxt[i]
+            if j >= 0:
+                left[j] -= 1
+                if left[j] == 0:
+                    seq.append(j)
+        if len(seq) < n:
+            return None, 1e18, []
+        total, held = 0.0, []
+        for u in range(len(cases)):
+            pu, hu, at = pres[u], holds[u], [0.0] * n
+            for i in seq:
+                j = prv[i]
+                t = at[j] + hu[j] if j >= 0 else 0.0
+                for d, l in pu[i]:
+                    if at[d] + l > t:
+                        t = at[d] + l
+                at[i] = t
+            fin = max(ends, key=lambda i: at[i] + costs[u][i])
+            total += at[fin] + costs[u][fin]
+            if u == 0:
+                times = at
+            while u == pick and at[fin] > 0.0:
+                j = prv[fin]
+                if j >= 0 and at[j] + hu[j] == at[fin]:
+                    held.append((fin, j))
+                    fin = j
+                else:
+                    fin = max(pu[fin], key=lambda e: at[e[0]] + e[1])[0]
+        return times, total / len(cases), held
+    at, end, held = ordered(key, 0)
+    best = (at0, 1e18, at0)
+    for it in range(CFG["swaps"] if held else 0):
+        i, j = held[rnd(len(held))]
+        b = list(key)
+        far = (0.01, 0.01, 200.0, 1000.0)[rnd(4)]
+        if rnd(2):
+            b[slot[i]] = key[slot[j]] + shift[j] - far - shift[i]
+        else:
+            b[slot[j]] = key[slot[i]] + shift[i] + far - shift[j]
+        at, e, held2 = ordered(b, rnd(len(cases)))
+        if e <= end + CFG["tol3"] * (1 - it / CFG["swaps"]) * rnd(100) / 100.0:
+            key, end, held = b, e, held2
+            if end < best[1]:
+                best = ([key[slot[u]] + shift[u] for u in range(n)], end, at)
+    order = {}
+    for i in sorted(range(n), key=lambda i: (best[0][i], i)):
+        order.setdefault(q_of[i], []).append(i)
+        ops[i]["t"] = best[2][i]
+    return order, best[1]
 
 
 def build(g, core, T, topo, rank, rt):
     ops, lastw, readers, lock = [], {}, {}, {}
-    grp = [0, 100000]
+    blk = [-1]
     V, A, PE = g.vector, g.scalar, g.tensor
-    CYC, GATH, RELU, ACTM, PA, RS = CFG["cyc"], CFG["gath"], CFG["relu"], CFG["actm"], CFG["pa"], CFG["rs"]
+    CYC, GATH = CFG["cyc"], CFG["gath"]
 
     def add(q, fn, cost, r=(), w=(), bank=(), sem=None, hold=None, after=()):
         i = len(ops)
         deps = set(after)
         for t in r:
-            if t in lastw:
-                deps.add(lastw[t])
+            deps.update(lastw.get(t, ()))
         for t in w:
-            if t in lastw:
-                deps.add(lastw[t])
+            deps.update(lastw.get(t, ()))
             deps.update(readers.get(t, ()))
         for b in bank:
             users = lock.setdefault(b, [])
@@ -164,11 +277,10 @@ def build(g, core, T, topo, rank, rt):
         for t in r:
             readers.setdefault(t, []).append(i)
         for t in w:
-            lastw[t] = i
+            lastw[t] = [i]
             readers[t] = []
         deps.discard(i)
-        ops.append({"q": q, "fn": fn, "cost": cost, "deps": sorted(deps), "sem": sem, "hold": cost if hold is None else hold,
-                    "grp": grp[0], "typ": i - grp[1]})
+        ops.append({"q": q, "fn": fn, "cost": cost, "deps": sorted(deps), "sem": sem, "hold": cost if hold is None else hold, "blk": blk[0]})
         return i
 
     def vc(cyc):
@@ -185,9 +297,6 @@ def build(g, core, T, topo, rank, rt):
     def cp(out, in_, cyc, r, w, bank=()):
         return add("V", lambda: V.tensor_copy(out, in_), vc(cyc), r, w, bank)
 
-    def ms(out, val, cyc, w):
-        return add("V", lambda: V.memset(out, val), vc(cyc), (), w)
-
     def scan(out, d0, d1, o0, o1, r, w):
         return add("V", lambda: V.tensor_tensor_scan(out, d0, d1, 0.0, o0, o1), vc(N), r, w)
 
@@ -197,22 +306,26 @@ def build(g, core, T, topo, rank, rt):
     def act(out, in_, f, cyc, r, w, bank=(), **kw):
         return add("A", lambda: A.activation(out, in_, f, **kw), CFG["oa"] + max(64.0, cyc) * CYC, r, w, bank)
 
-    def mm(lst, r, w, bank):
+    def mm(lst, r, w, bank, wide=1):
         def fn():
             ins = None
             for (o, l, x, st, sp) in lst:
                 ins = PE.matmul(o, l, x, st, sp)
             return ins
-        return add("P", fn, 40.0 + sum(max(64, m[2].shape[1]) * CFG["pe"] for m in lst), r, w, bank)
+        hold = sum(max(64, m[2].shape[1]) * CFG["pe"] * wide for m in lst)
+        return add("P", fn, hold + 50.0, r, w, [bank], hold=hold)
 
-    def lin(bank, terms, r, w):
-        return mm([(o, T.ih[:, 0:128] if sg > 0 else T.ih[:, 128:256], x, bool(a), bool(b)) for (o, sg, x, a, b) in terms], list(r) + ["ih"], w, [bank])
+    def lin(bank, terms, r, w, start=False, stop=False):
+        return mm([(o, m, x, start and j == 0, stop and j == len(terms) - 1) for j, (o, m, x) in enumerate(terms)], r, w, bank)
 
-    def dma(q, out, in_, sem, r, w):
+    def zero(bank, a, n, w):
+        return lin(bank, [(T[bank][:, a:a + n], T.zb[:, 0:128], T.zb[:, 0:n])], ["zb"], w, True)
+
+    def dma(q, out, in_, sem, total, r, w):
         e = g.sync if q == "S" else g.scalar
-        return add(q, lambda: e.dma_start(out, in_), 2500.0, r, w, sem=(sem, 16), hold=60.0)
+        return add(q, lambda: e.dma_start(out, in_), 2500.0, r, w, sem=(sem, total, 16), hold=60.0)
 
-    def iota(out, pat, base, mult, cyc, w, small=False):
+    def iota(out, pat, base, mult, cyc, w, small=True):
         if small:
             return add("G", lambda: g.iota(out, pat, base, mult, allow_small_or_imprecise_dtypes=True), 130.0 + 2 * cyc, (), w)
         return add("G", lambda: g.iota(out, pat, base, mult), 130.0 + 2 * cyc, (), w)
@@ -220,261 +333,306 @@ def build(g, core, T, topo, rank, rt):
     def col(j):
         return T.cf[:, j:j + 1]
 
-    dma("S", T.homi[:], T.hom[:], "ld0", (), ["homi"])
-    dma("A", T.xs[:, 0:1024], T.x[:, 0:1024], "ld1", (), ["xa"])
-    dma("S", T.xs[:, 1024:2048], T.x[:, 1024:2048], "ld2", (), ["xb"])
-    dma("A", T.thi[:, 0:1], T.th[:], "ld3", (), ["thi"])
-    X = ["xa", "xb"]
-    iota(T.pi[:, 0:1], [[0, 1]], 0, 1, 1, ["pi0"])
-    iota(T.ji[:], [[1, 144]], 0, 0, 144, ["ji"])
-    iota(T.lci[:, 0:2 * NB], [[256, 2], [512, NB]], 16, 0, 8, ["lci"], True)
-    ts(T.pi[:, 1:2], T.pi[:, 0:1], 112, None, ALU.bitwise_and, None, 1, ["pi0"], ["pi1"])
-    ts(T.pi[:, 2:3], T.pi[:, 0:1], 15, None, ALU.bitwise_and, None, 1, ["pi0"], ["pi2"])
-    ts(T.pi[:, 3:4], T.pi[:, 0:1], 16, None, ALU.bitwise_and, None, 1, ["pi0"], ["pi3"])
-    cp(T.cf[:, 0:4], T.pi[:, 0:4], 4, ["pi0", "pi1", "pi2", "pi3"], ["c0"])
-    cP, cG, cK, cH = col(0), col(1), col(2), col(3)
-    cp(T.jf[:], T.ji[:], 144, ["ji"], ["jf"])
-    ts(T.jg[:], T.ji[:, 0:128], 112, None, ALU.bitwise_and, None, 128, ["ji"], ["jg"])
-    ts(T.jk[:], T.ji[:, 0:N], 15, None, ALU.bitwise_and, None, N, ["ji"], ["jk"])
-    ts(T.rst[:], T.jk[:], 15.0, None, ALU.is_equal, None, N, ["jk"], ["rst"])
-    ts(T.keep[:], T.jk[:], 0.0, None, ALU.not_equal, None, N, ["jk"], ["keep"])
-    ts(T.wb[:], T.jf[:], cG, 15.0, ALU.subtract, ALU.is_equal, 144, ["jf", "c0"], ["wb"])
-    if RELU:
-        ts(T.wn[:], T.wb[:], -1.0, None, ALU.mult, None, 72, ["wb"], ["wn"])
-    for buf, nm in ((T.ib, "ib"), (T.ih, "ih")):
-        ts(buf[:, 0:128], T.jf[:, 0:128], cP, 1.0, ALU.is_equal, ALU.mult, 128, ["jf", "c0"], [nm])
-        ts(buf[:, 128:256], T.jf[:, 0:128], cP, -1.0, ALU.is_equal, ALU.mult, 128, ["jf", "c0"], [nm])
-    ms(T.zb[:], 0.0, 96, ["zb"])
-    ms(T.zf[:], 0.0, N, ["zf"])
-    ms(T.m192[:], -192.0, 64, ["m192"])
-    ms(T.ka[:], 2048.0, 64, ["ka"])
-    for j, (lim, op, val) in enumerate(((3.0, ALU.is_lt, 4096.0), (3.0, ALU.is_lt, -4096.0), (13.0, ALU.is_ge, 4096.0), (13.0, ALU.is_ge, -4096.0))):
-        ts(col(4 + j), cK, lim, val, op, ALU.mult, 1, ["c0"], ["c%d" % (4 + j)])
-        ts(T.zm[:, 128 * j:128 * j + 128], T.jg[:], cG, col(4 + j), ALU.is_equal, ALU.mult, 128, ["jg", "c0", "c%d" % (4 + j)], ["zm"])
-    ts(col(8), cK, 3.0, 16.0, ALU.is_ge, ALU.mult, 1, ["c0"], ["c8"])
-    ts(col(9), cK, 12.0, col(8), ALU.is_le, ALU.mult, 1, ["c0", "c8"], ["c9"])
-    ts(col(10), cK, 3.0, -1.0e7, ALU.is_lt, ALU.mult, 1, ["c0"], ["c10"])
-    ts(col(12), col(10), 1.0, None, ALU.add, None, 1, ["c10"], ["c12"])
-    ts(col(15), cK, 592.0, -7.5, ALU.mult, ALU.add, 1, ["c0"], ["c15"])
-    for jh in range(2):
-        ts(col(16 + jh), cH, 16.0 * jh, -1.0, ALU.is_equal, ALU.mult, 1, ["c0"], ["c%d" % (16 + jh)])
-    ts(col(18), cP, 16.0, None, ALU.add, None, 1, ["c0"], ["c18"])
-    ts(col(19), cP, -16.0, None, ALU.add, None, 1, ["c0"], ["c19"])
-    for jh in range(2):
-        for h in range(2):
-            sc = cP if h == jh else col(18 if h > jh else 19)
-            j = 2 * jh + h
-            ts(T.pm[:, 128 * j:128 * j + 128], T.jf[:, 0:128], sc, col(16 + jh), ALU.is_equal, ALU.mult, 128,
-               ["jf", "c0", "c16", "c17", "c18", "c19"], ["pm"])
-    ts(col(20), cK, 16.0, None, ALU.mult, None, 1, ["c0"], ["c20"])
-    ts(T.lc[:, 0:2 * NB], T.lci[:, 0:2 * NB], col(20), None, ALU.add, None, 8, ["lci", "c20"], ["lc"])
-    ts(col(21), cP, 0.0, 6144.0, ALU.is_equal, ALU.mult, 1, ["c0"], ["c21"])
-    ts(col(22), cP, 1.0, None, ALU.is_equal, None, 1, ["c0"], ["c22"])
+    def ps(buf, j, m=1):
+        return buf[:, j * N:(j + m) * N]
+
+    h0 = dma("S", T.homi[:, 0:TT], T.hom[:, 0:TT], "lh0", 16, (), [("homi", 0)])
+    xl = [dma("AS"[c], T.xs[:, LK * c:LK * c + LK], T.x[:, LK * c:LK * c + LK], "lx%d" % c, 16, (), [("x", c)]) for c in range(2)]
+    dma("A", T.homi[:, TT:4 * TT], T.hom[:, TT:4 * TT], "lh1", 16, (), [("homi", s) for s in (1, 2, 3)])
+    dma("S", T.thi[:, 0:1], T.th[:], "lt", 16, (), ["thi"])
+    X, xw = [("x", 0), ("x", 1)], T.xs[:, 0:WX]
+    for c in range(2):
+        for s in (0,) + CFG["role"]:
+            a = ocol(0, c, s)
+            cp(T.off[:, a:a + N], T.homi[:, TT * s + N * c:TT * s + N * c + N], N, [("homi", s)], [("off", 0, c, s)])
+    iota(T.dj[:], [[1, 128]], 0, -1, 128, ["dj"])
+    iota(T.pi[:, 0:1], [[0, 1]], 0, 1, 1, ["pi0"], False)
+    iota(T.zb[:], [[0, 384]], 0, 0, 384, ["zb"])
+    iota(T.j8[:], [[0, 2], [1, 8], [0, 2]], 0, 0, 32, ["j8"])
+    iota(T.wm[:], [[0, 24], [1, 2], [0, 8]], 0, 0, 384, ["jw"])
+    iota(T.jb[:], [[1, N]], 0, 0, N, ["jb"])
+    iota(T.jg[:], [[1, 8], [0, 16]], 0, 0, 128, ["jg"])
+    iota(T.ka[0:2, :], [[0, 128]], int(OFFK), 1024 - int(OFFK), 128, ["ka"])
     for p in (1, 2):
-        ts(col(23), col(22), float(p), col(21), ALU.mult, ALU.add, 1, ["c21", "c22"], ["c23"])
-        ts(T.kb[:, 2 * (p - 1) * N:2 * p * N], T.zb[:, 0:2 * N], col(23), None, ALU.add, None, N, ["zb", "c23"], ["kb"])
-    cp(T.thr[:, 0:1], T.thi[:, 0:1], 1, ["thi"], ["thr"])
-    for s in range(4):
-        cp(T.off[:, s * TT:(s + 1) * TT], T.homi[:, s * TT:(s + 1) * TT], TT, ["homi"], [("off", 0, c, s) for c in range(NCH)])
+        iota(T.kb[0:2, 128 * p - 128:128 * p], [[0, 128]], 1, 2 * p, 128, [("kb", p)])
+    iota(T.one[:], [[0, N]], 1, 0, N, ["one"])
+    for buf, nm, lim in ((T.kp3, "kp3", 3), (T.keep, "keep", 1)):
+        add("G", lambda buf=buf, lim=lim: g.affine_select(buf[:], T.one[:], [[0, 4], [1, 16]], ALU.is_ge, 0.0, -lim, 0), 170.0 + 2 * N, ["one"], [nm])
+    iota(T.lci[:, 0:4], [[256, 2], [512, 2]], 16, 0, 4, ["lci"])
+    iota(T.m192[:], [[0, N]], -192, 0, N, ["m192"])
+    for j, (sh, msk) in enumerate(((4, 7), (0, 15), (0, 16), (1, 63), (0, 1))):
+        ts(T.pi[:, j + 1:j + 2], T.pi[:, 0:1], sh, msk, ALU.arith_shift_right, ALU.bitwise_and, 1, ["pi0"], ["pi%d" % (j + 1)])
+    cp(T.cf[:, 0:6], T.pi[:, 0:6], 8, ["pi%d" % j for j in range(6)], ["c0"])
+    cP, cG, cK, cH, cT, cO = [col(j) for j in range(6)]
+    for buf, nm, val in ((T.ib, "ib", 1.0), (T.ih, "ih", 1.0), (T.i16, "i16", 16.0)):
+        ts(buf[:, 0:128], T.dj[:], 0.0, val, ALU.is_equal, ALU.mult, 64, ["dj"], [nm + "+"])
+        ts(buf[:, 128:256], T.dj[:], 0.0, -val, ALU.is_equal, ALU.mult, 64, ["dj"], [nm + "-"])
+    IB, NB, IH, NH, I16, N16 = T.ib[:, 0:128], T.ib[:, 128:256], T.ih[:, 0:128], T.ih[:, 128:256], T.i16[:, 0:128], T.i16[:, 128:256]
+    for a, b, val in ((0, 32, -0.5), (32, 48, 1.0), (48, 64, 0.5)):
+        ts(T.gm[:, a:b], T.j8[:, 0:b - a], cG, val, ALU.is_equal, ALU.mult, 16, ["j8", "c0"], [("gm", a)])
+    GM = [("gm", a) for a in (0, 32, 48)]
+    ts(T.em[:], T.jb[:], cT, None, ALU.is_equal, None, 64, ["jb", "c0"], ["em"])
+    ts(T.wm[:], T.wm[:], cO, None, ALU.is_equal, None, 192, ["jw", "c0"], ["wm"])
+    for j, (lim, op) in enumerate(((3.0, ALU.is_lt), (13.0, ALU.is_ge))):
+        ts(col(6 + j), cK, lim, 8192.0, op, ALU.mult, 1, ["c0"], [("c", 6 + j)])
+        ts(T.zm[:, 128 * j:128 * j + 128], T.jg[:], cG, col(6 + j), ALU.is_equal, ALU.mult, 64, ["jg", "c0", ("c", 6 + j)], [("zm", j)])
+    act(col(8), col(7), AF.Identity, 1, [("c", 7)], [("c", 8)], bias=M2048, scale=4.0)
+    if CFG["mov"]:
+        ts(T.zm[:, 256:512], T.zm[:, 0:256], -1.0, None, ALU.mult, None, 128, [("zm", 0), ("zm", 1)], [("zm", 2), ("zm", 3)])
+        iota(T.jw[:], [[1, 144]], -15, 0, 144, ["jv"])
+        act(col(10), cG, AF.Identity, 1, ["c0"], [("c", 10)], scale=16.0)
+        for j, val in enumerate((0.5, 1.0, -0.5)):
+            ts(T.wb[:, 144 * j:144 * j + 144], T.jw[:], col(10), val, ALU.is_equal, ALU.mult, 72, ["jv", ("c", 10), "wb"], ["wb"])
+    if CFG["dqa"]:
+        act(col(9), col(7), AF.Identity, 1, [("c", 7)], [("c", 9)], bias=-M2048, scale=-4.0)
+    for c in CFG["dei"]:
+        add("V", lambda c=c: V.memset(T["wd%d" % c][:], 0.0), vc(224), (), [("w0", c)])
+    for jh in range(2):
+        act(col(13 + jh), cH, AF.Identity, 1, ["c0"], [("c", 13 + jh)], bias=jh - 1.0, scale=(1 - 2 * jh) / 16.0)
+        for h in range(2):
+            j = 2 * jh + h
+            ts(T.pm[:, 128 * j:128 * j + 128], T.dj[:], 16.0 * (h - jh), col(13 + jh), ALU.is_equal, ALU.mult, 64, ["dj", ("c", 13 + jh)], [("pm", j)])
+    act(col(15), cK, AF.Identity, 1, ["c0"], [("c", 15)], scale=16.0)
+    act(T.lc[:, 0:4], T.lci[:, 0:4], AF.Identity, 4, ["lci", ("c", 15)], ["lc"], bias=col(15))
+    act(col(18), cK, AF.Identity, 1, ["c0"], [("c", 18)], scale=592.0)
+    ts(T.dk[:], T.dj[:], 0.0, col(18), ALU.is_equal, ALU.mult, 64, ["dj", ("c", 18)], ["dk"])
+    act(col(19), cK, AF.Relu, 1, ["c0"], [("c", 19)], bias=-7.0, scale=0.5)
+    ts(T.sel[:], T.jg[:], cG, col(19), ALU.is_equal, ALU.mult, 64, ["jg", "c0", ("c", 19)], ["sel"])
+    ts(T.thf[:, 0:1], T.thi[:, 0:1], 0.5, 1024.0, ALU.mult, ALU.add, 1, ["thi"], ["thr"])
+    act(T.thf[:, 1:2], T.thf[:, 0:1], AF.Identity, 1, ["thr"], ["th3"], bias=7.75)
 
-    nd = [0]
-    sent = [0]
+    sent, stores, adds = [0], [], []
     for v in range(VI):
-        grp[1] = len(ops)
-        for c in range(NCH):
-            grp[0] = v * NCH + c
+        for c in range(2):
+            blk[0] = v * 2 + c
+            U = {nm: T[nm + str(c)] for nm in OWN}
 
-            def sl(buf, k, j=0, m=1):
-                return buf[:, (c * k + j) * N:(c * k + j + m) * N]
+            def k_(*nms):
+                return [(nm, c) for nm in nms]
 
-            def tk(name):
-                return (name, c)
+            def ga(j, a, n, step=1):
+                return U["ga"][:, j * LK + a:j * LK + a + n:step]
 
-            def ps(buf, j, m=1):
-                return buf[:, j * N:(j + m) * N]
+            def gt(j, a, n):
+                return [("ga", c, j, u) for u in range(a // 128, (a + n) // 128)]
 
-            def rev(buf, a):
-                return buf[:, a + N - 1:(a - 1 if a else None):-1]
+            def ab(ar, a, n, step=1):
+                return U["ab"][:, ar * LK + a:ar * LK + a + n:step]
 
-            def st(u, j, m=1):
-                a = ((u % 2) * NCH + c) * 7 * N + j * N
-                return T.sh[:, a:a + m * N]
-            SH = [st(v, 0), st(v, 4), st(v, 5), st(v, 6)]
-            shk, s0k = ("sh", v % 2, c), ("s0", v % 2, c)
-            if v > 0:
-                a = ocol(v, c, 1)
-                cp(st(v, 4, 3), T.off[:, a:a + 3 * N], 1.5 * N, [("off", v, c, s) for s in (1, 2, 3)], [shk])
+            def abt(ar, a=0, n=LK):
+                return [("ab", c, ar, hf) for hf in range(a // 512, (a + n) // 512)]
+
+            def ind(s, a, n):
+                o = ocol(v, c, s) + a // 16
+                return xw.indirect(T.off[:, o:o + n // 16])
+            S1, S2, S3, S0 = [ps(U["sh"], j) for j in range(4)]
+            a = ocol(v, c, 1)
+            cp(ps(U["sh"], 0, 4), T.off[:, a:a + 4 * N], 2 * N, [("off", v, c, s) for s in range(4)], k_("sh"))
+            PV, PB = CFG["pv"], CFG["pb"]
+            a = 0
+            for n in CFG["pa"]:
+                act(ga(0, a, n), ind(0, a, n), AF.Identity, n * GATH, X + [("off", v, c, 0)], gt(0, a, n), scale=-1.0)
+                a += n
+            for s, pieces in zip(CFG["role"], PV):
+                a = 0
+                if (c, s) in CFG["dma"]:
+                    for n in CFG["pd"]:
+                        act(ga(s, a, n), ind(s, a, n), AF.Identity, n * GATH, X + [("off", v, c, s)], gt(s, a, n))
+                        add("G", lambda o=ga(s, a, n), i=ga(0, a, n): g.dma_start(o, i, accum_op=ALU.add), CFG["dlat"], gt(0, a, n), gt(s, a, n),
+                            sem=("d%d" % len(adds), 16, 16), hold=1000.0)
+                        adds.append(a)
+                        a += n
+                    continue
+                for n in pieces:
+                    if (c, s, a // 512) in CFG["plain"]:
+                        act(ga(s, a, n), ind(s, a, n), AF.Identity, n * GATH, X + [("off", v, c, s)], gt(s, a, n))
+                        a += n
+                        continue
+                    tt(ga(s, a, n), ind(s, a, n), ga(0, a, n), ALU.add, n * GATH, X + [("off", v, c, s)] + gt(0, a, n), gt(s, a, n))
+                    a += n
+            done = [("CT", 0)]
+            dei = c in CFG["dei"]
+            mov = c in CFG["mov"]
+            zero("pc", 0, 192 if dei or mov else 384, done + ["CO"])
+
+            def sums(view, toks, p, rhs, last=False, kind=0):
+                o, n = (0, 384) if p == 0 else (128 * (p - 1), 128)
+                if mov:
+                    for k0 in range(0, 16, 2 * CFG["rs"]):
+                        w, end = [("CT", len(done))], last and k0 + 2 * CFG["rs"] == 16
+                        mm([(ps(T.pc, (p + 2) % 3), T.wb[:, 144 * kind + 15 - k:144 * kind + 143 - k], view(k, 16), False, end and k == 15)
+                            for k in range(k0, k0 + 2 * CFG["rs"])], ["wb"] + toks + (done if end else done[:1]), w, "pc")
+                        done.extend(w)
+                    return
+                if dei:
+                    o, n, rhs = o // 2, n // 2, T.gm[:, 0:48:2] if p == 0 else T.gm[:, 48:64:2]
+                for k0 in range(0, 8, CFG["rs"]):
+                    w, end = [("CT", len(done))], last and k0 + CFG["rs"] == 8
+                    mm([(T.pc[:, o + k:o + n:8], view(k), rhs, False, end and k == 7) for k in range(k0, k0 + CFG["rs"])],
+                       GM + toks + (done if end else done[:1]), w, "pc")
+                    done.extend(w)
+
+            def plain(p):
+                return T.gm[:, 0:48] if p == 0 else T.gm[:, 48:64]
+            for s in CFG["role"]:
+                if (c, s) in CFG["relu"]:
+                    for a in (0, 512):
+                        ts(ab(s - 1, a, 512), ga(s, a, 512), 0.0, None, ALU.max, None, 256, gt(s, a, 512), abt(s - 1, a, 512))
+                    sums(lambda k, st=8: ga(s, k, LK - k, st), gt(s, 0, LK), s - 1, T.gm[:, 0:16], kind=2)
+                    sums(lambda k, st=8: ab(s - 1, k, LK - k, st), abt(s - 1), s - 1, T.gm[:, 32:48], kind=1)
+                else:
+                    for a in range(0, LK, PB):
+                        if (c, s, a // 512) in CFG["plain"]:
+                            bk = "pd%d" % (a // 512)
+                            for u in (0, s):
+                                lin(bk, [(T[bk][:, 0:512], IB, ga(u, a, 512))], ["ib+"] + gt(u, a, 512), [bk], u == 0, u == s)
+                            act(ab(s - 1, a, 512), T[bk][:, 0:512], AF.Abs, 512, [bk], abt(s - 1, a, 512), [bk])
+                        elif dei:
+                            act(ab(s - 1, a, 512), ga(s, a // 512, LK - a // 512, 2), AF.Abs, 512, gt(s, 0, LK), abt(s - 1, a, 512))
+                        else:
+                            act(ab(s - 1, a, PB), ga(s, a, PB), AF.Abs, PB, gt(s, a, PB), abt(s - 1, a, PB))
+                    sums(lambda k, st=8: ab(s - 1, k, LK - k, st), abt(s - 1), s - 1, plain(s - 1))
+            for j, (s, t) in enumerate(CFG["pairs"][c]):
+                for hf in range(2):
+                    bk, a = "pd%d" % hf, 512 * hf
+                    terms = [(m, 0) for m, u in ((IB, s), (NB, t)) if (c, u, hf) in CFG["plain"]] + [(IB, s), (NB, t)]
+                    for m, u in terms:
+                        lin(bk, [(T[bk][:, 0:512], m, ga(u, hf, LK - hf, 2) if dei else ga(u, a, 512))],
+                            ["ib+", "ib-"] + (gt(u, 0, LK) if dei else gt(u, a, 512)), [bk], u == terms[0][1], u == t)
+                    act(ab(3 + j, a, 512), T[bk][:, 0:512], AF.Abs, 512, [bk], abt(3 + j, a, 512), [bk])
+                sums(lambda k, st=8: ab(3 + j, k, LK - k, st), abt(3 + j), 5 - s - t, plain(5 - s - t), j == 2)
+            S23 = ps(U["sh"], 1, 2)
+            IHS = ["ih+", "ih-"] + k_("sh")
+            mm([(ps(T.r1, 0), IH, S2, True, False), (ps(T.r1, 0), NH, S1, False, True), (ps(T.r1, 1), IH, S2, True, False), (ps(T.r1, 1), NH, S3, False, True)],
+               IHS, ["R1"], "r1")
+            if dei:
+                cp(U["wd"][:, 2:386:2], T.pc[:, 0:192], 192, done + k_("w0"), k_("wt"), ["pc"])
+                mm([(ps(T.pc, p), U["wd"][:, 2 - e + 128 * p:130 - e + 128 * p], ps(T.ih, e), e == 0, e == 1) for p in range(3) for e in range(2)],
+                   k_("wt") + ["ih+"], ["CO"] + done, "pc")
+            elif not mov:
+                tt(U["wt"][:], T.pc[:, 0:384], T.wm[:], ALU.mult, 384, done + ["wm"], k_("wt"), ["pc"])
+                mm([(ps(T.pc, p), ps(U["wt"], 2 * p, 2), T.em[:], True, True) for p in range(3)], k_("wt") + ["em"], ["CO"] + done, "pc")
+            CO, nch = (done, 3) if mov else (["CO"], 2)
+            cp(ps(U["ch"], 0, nch), ps(T.pc, 0, nch), nch * N, CO, k_("ch"), ["pc"])
+            act(ps(T.r1, 4), ps(T.pc, 2), AF.Identity, N, CO + ["thr"], ["Y"], ["pc", "r1"], bias=T.thf[:, 0:1], scale=-1.0 if mov else -0.5)
+            lin("pk", [(ps(T.pk, 0, 4), T.ka[0:2, :], T.kb[0:2, :])], ["ka", ("kb", 1), ("kb", 2)], ["K"], True)
+            terms = [(T.zm[:, 256:384], T.zm[:, 384:512], 2), (NH, NH, 2)] * mov
+            lin("pk", [(ps(T.pk, 2 * p + e), m[e], ps(U["ch"], u)) for p in range(2) for e in range(2)
+                       for *m, u in terms[:1] + [(T.zm[:, 0:128], T.zm[:, 128:256], p), (IH, IH, p)] + terms[1:]],
+                [("zm", j) for j in range(4 if mov else 2)] + ["ih+", "ih-"] + k_("ch"), ["K"], False, True)
+            ts(U["m1"][:], ps(T.pk, 0, 2), OFFK + 1024.0, None, ALU.min, None, 128, ["K"], k_("m1"), ["pk"])
+            tt(U["mk"][:], ps(T.pk, 2, 2), U["m1"][:], ALU.min, 128, ["K"] + k_("m1"), k_("mk"), ["pk"])
+            ts(U["tk"][:], U["mk"][:], 8191, None, ALU.bitwise_and, None, 128, k_("mk"), k_("tk"))
+            tt(U["dt"][:], ps(U["tk"], 0), ps(U["tk"], 1), ALU.subtract, 128, k_("tk"), k_("dt"))
+            if c in CFG["dqa"]:
+                act(U["uu"][:], U["dt"][:], AF.Identity, N, k_("dt"), k_("uu"), bias=M2048)
+                act(ps(T.pk, 4), U["uu"][:], AF.Identity, N, k_("uu") + [("c", 9)], ["DQ"], ["pk"], bias=col(9))
             else:
-                grp[1] += 3
-                for s in range(4):
-                    cp(SH[s], T.homi[:, s * TT + c * N:s * TT + (c + 1) * N], N, ["homi"], [shk if s else s0k])
-            c0 = c * 16 * N
-            pieces = list(range(c0, c0 + 16 * N, PC))
-            mm([(T.pc[:, 0:3 * N], T.zb[:, 0:128], T.zb[:, 0:3 * N], True, False)], ["zb"], ["C"], ["pc"])
-
-            def ind(s, a):
-                o = ocol(v, c, s) + (a - c0) // 16
-                return T.xs[:, 0:WX].indirect(T.off[:, o:o + PC // 16])
-            for a in pieces:
-                act(T.p0[:, a:a + PC], ind(0, a), AF.Identity, PC * GATH, X + [("off", v, c, 0)], [("p0", a)])
-            for s in (2, 1, 3):
-                for a in pieces:
-                    o = (s - 1) * WX + a
-                    tt(T.dd[:, o:o + PC], ind(s, a), T.p0[:, a:a + PC], ALU.subtract, PC * GATH, X + [("off", v, c, s), ("p0", a)], [("dd", s, a)])
-                for a in range(c0, c0 + 16 * N, PA):
-                    o = (s - 1) * WX + a
-                    rr, ww = [("dd", s, b) for b in range(a, a + PA, PC)], [("ab", s - 1, b) for b in range(a, a + PA, PC)]
-                    if s in RELU:
-                        ts(T.ab[:, o:o + PA], T.dd[:, o:o + PA], 0.0, 2.0, ALU.max, ALU.mult, PA / 2, rr, ww)
-                    else:
-                        act(T.ab[:, o:o + PA], T.dd[:, o:o + PA], AF.Abs, PA, rr, ww)
-                for p, (s1, s2) in {2: (), 1: ((2, (1, 2)),), 3: ((1, (1, 3)), (0, (2, 3)))}[s]:
-                    for a in pieces:
-                        bk = "pd%d" % (nd[0] % 2)
-                        nd[0] += 1
-                        o1, o2, o = (s1 - 1) * WX + a, (s2 - 1) * WX + a, (3 + p) * WX + a
-                        mm([(T[bk][:, 0:PC], T.ib[:, 0:128], T.dd[:, o1:o1 + PC], True, False),
-                            (T[bk][:, 0:PC], T.ib[:, 128:256], T.dd[:, o2:o2 + PC], False, True)], ["ib", ("dd", s1, a), ("dd", s2, a)], [bk], [bk])
-                        act(T.ab[:, o:o + PC], T[bk][:, 0:PC], AF.Abs, PC, [bk], [("ab", 3 + p, a)], [bk])
-            arrs = [(s - 1, T.dd, T.wn, ["wn"] + [("dd", s, a) for a in pieces]) for s in RELU]
-            arrs += [(ar, T.ab, T.wb, ["wb"] + [("ab", ar, a) for a in pieces]) for ar in (1, 0, 5, 2, 4, 3)]
-            for j, (ar, buf, wm, rr) in enumerate(arrs):
-                p, base = ar % 3, ar * WX + c0
-                for k0 in range(0, 16, RS):
-                    last = j == len(arrs) - 1 and k0 + RS == 16
-                    mm([(ps(T.pc, p), wm[:, 15 - k:143 - k], buf[:, base + k:base + 16 * N:16], False, last and k == 15)
-                        for k in range(k0, k0 + RS)], rr + ([] if last else ["C"]), ["C"] if last else [], ["pc"])
-            cp(sl(T.ch, 3, 0, 3), ps(T.pc, 0, 3), 3 * N, ["C"], [tk("ch")], ["pc"])
-            for e in range(2 if "k0" in ACTM else 1):
-                act(sl(T.k0, 2, e), ps(T.pc, 0), AF.Identity, N, ["C"], [("k0", c, e)], ["pc"], bias=OFFK)
-            mm([(ps(T.pk, 0, 4), T.ka[:], T.kb[:], True, False)], ["ka", "kb"], ["K", "K1", "K2"], ["pk"])
-            lst = []
-            for p in (1, 2):
-                for e in range(2):
-                    o = ps(T.pk, 2 * (p - 1) + e)
-                    lst += [(o, T.zm[:, 256 * e:256 * e + 128], sl(T.ch, 3, p), False, False),
-                            (o, T.zm[:, 256 * e + 128:256 * e + 256], sl(T.ch, 3, 0), False, False),
-                            (o, T.ih[:, 0:128], sl(T.ch, 3, p), False, p == 2 and e == 1)]
-            mm(lst, ["zm", "ih", tk("ch")], ["K"], ["pk"])
-            if "k0" in ACTM:
-                tt(sl(T.m1, 2, 0, 2), ps(T.pk, 0, 2), sl(T.k0, 2, 0, 2), ALU.min, 2 * N, ["K", ("k0", c, 0), ("k0", c, 1)], [("m1", c, 0), ("m1", c, 1)], ["pk"])
-            else:
-                for e in range(2):
-                    tt(sl(T.m1, 2, e), ps(T.pk, e), sl(T.k0, 2, 0), ALU.min, N, ["K", ("k0", c, 0)], [("m1", c, e)], ["pk"])
-            tt(sl(T.mk, 2, 0, 2), ps(T.pk, 2, 2), sl(T.m1, 2, 0, 2), ALU.min, 2 * N, ["K", ("m1", c, 0), ("m1", c, 1)], [tk("mk")], ["pk"])
-            ts(sl(T.xi, 4, 0, 2), sl(T.mk, 2, 0, 2), 2047, None, ALU.bitwise_and, None, 2 * N, [tk("mk")], [tk("xc")])
-            tt(sl(T.df, 2, 0), sl(T.xi, 4, 0), sl(T.xi, 4, 1), ALU.subtract, 2 * N, [tk("xc")], [tk("D")])
-            ts(sl(T.xi, 4, 2, 2), sl(T.mk, 2, 0, 2), 11, 3, ALU.arith_shift_right, ALU.bitwise_and, 2 * N, [tk("mk")], [tk("xp")])
-            tt(sl(T.df, 2, 1), sl(T.xi, 4, 2), sl(T.xi, 4, 3), ALU.subtract, 2 * N, [tk("xp")], [tk("dp")])
-            if "dq" in ACTM:
-                act(sl(T.dq, 1), sl(T.df, 2, 0), AF.Identity, N, [tk("D"), "c9", "c12"], [tk("dq")], bias=col(12), scale=col(9))
-            else:
-                ts(sl(T.dq, 1), sl(T.df, 2, 0), col(9), col(12), ALU.mult, ALU.add, N, [tk("D"), "c9", "c12"], [tk("dq")])
-            turn(sl(T.dv, 1), sl(T.dq, 1), [tk("dq")], [tk("dv")])
-            scan(sl(T.uu, 1), sl(T.dv, 1), T.zf[:], ALU.add, ALU.max, [tk("dv"), "zf"], [tk("uu")])
-            scan(rev(T.rt, c * N), rev(T.rst, 0), rev(T.uu, c * N), ALU.max, ALU.min, [tk("uu"), "rst"], [tk("rt")])
-            scan(sl(T.run, 1), T.keep[:], sl(T.rt, 1), ALU.mult, ALU.add, [tk("rt"), "keep"], [tk("run")])
-            lo = c * 2 * NB
-            mm([(T.pl[:, 0:2 * NB], T.ib[:, 0:128], T.lc[:, 0:2 * NB], True, False)], ["ib", "lc"], ["L"], ["pl"])
-            mm([(T.pl[:, jh * NB:(jh + 1) * NB], T.pm[:, 128 * (2 * jh + h):128 * (2 * jh + h + 1)],
-                 T.run[:, c * N + 16 * h + 15:(c + 1) * N:32], False, jh == 1 and h == 1) for jh in range(2) for h in range(2)],
-               ["pm", tk("run")], ["L"], ["pl"])
-            cp(T.lst[:, lo:lo + 2 * NB], T.pl[:, 0:2 * NB], 8, ["L"], [tk("lst")], ["pl"])
-            turn(ps(T.pk, 0), sl(T.rt, 1), [tk("rt")], ["K"], ["pk"])
-            tt(ps(T.pk, 2), ps(T.pk, 0), sl(T.df, 2, 1), ALU.mult, N, ["K", tk("dp")], ["K2"], ["pk"])
-            tt(sl(T.cp, 2, 1), sl(T.xi, 4, 2), ps(T.pk, 2), ALU.subtract, N, ["K2", tk("xp")], [tk("P")], ["pk"])
-            tt(ps(T.pk, 1), ps(T.pk, 0), sl(T.df, 2, 0), ALU.mult, N, ["K", tk("D")], ["K1"], ["pk"])
-            tt(sl(T.cp, 2, 0), sl(T.xi, 4, 0), ps(T.pk, 1), ALU.subtract, N, ["K1", tk("xc")], [tk("cp")], ["pk"])
-            ts(sl(T.sw, 1), ps(T.pk, 2), 0.0, None, ALU.not_equal, None, N, ["K2"], [tk("sw")], ["pk"])
-            if "fm" in ACTM:
-                act(sl(T.fm, 2, 0), sl(T.cp, 2, 1), AF.Relu, N, [tk("P")], [tk("f0")], bias=1.0, scale=-1.0)
-                act(sl(T.fm, 2, 1), sl(T.cp, 2, 1), AF.Relu, N, [tk("P")], [tk("f2")], bias=-1.0)
-            else:
-                ts(sl(T.fm, 2, 0), sl(T.cp, 2, 1), 0.0, None, ALU.is_equal, None, N, [tk("P")], [tk("f0")])
-                ts(sl(T.fm, 2, 1), sl(T.cp, 2, 1), 2.0, None, ALU.is_equal, None, N, [tk("P")], [tk("f2")])
-            ts(sl(T.ov, 1), sl(T.cp, 2, 0), T.thr[:, 0:1], 0.0625, ALU.is_gt, ALU.mult, N, [tk("cp"), "thr"], [tk("ov")])
-            F = [tk("f0"), tk("f2")]
+                ts(ps(T.pk, 4), U["dt"][:], M2048, col(8), ALU.add, ALU.subtract, N, k_("dt") + [("c", 8)], ["DQ"], ["pk"])
+            tt(U["dq"][:], U["dt"][:], ps(T.pk, 4), ALU.subtract, N, k_("dt") + ["DQ"], k_("dq"), ["pk"])
+            turn(U["dv"][:], U["dq"][:], k_("dq"), k_("dv"))
+            scan(U["uu"][:, ::-1], U["dv"][:, ::-1], T.one[:], ALU.add, ALU.min, k_("dv") + ["one"], k_("uu"))
+            scan(U["rt"][:], U["uu"][:], T.kp3[:], ALU.max, ALU.min, k_("uu") + ["kp3"], k_("rt"))
+            turn(ps(T.pk, 5), U["rt"][:], k_("rt"), ["RT"], ["pk"])
+            tt(ps(T.pk, 6), ps(T.pk, 5), U["dt"][:], ALU.mult, N, ["RT"] + k_("dt"), ["KK"], ["pk"])
+            tt(U["tf"][:], ps(U["tk"], 0), ps(T.pk, 6), ALU.subtract, N, ["KK"] + k_("tk"), k_("tf"), ["pk"])
+            act(U["junk"][:], ps(T.pk, 6), AF.Sign, N, ["KK"], k_("junk"), ["pk"])
             if v < VI - 1:
-                act(sl(T.sg, 2, 0), sl(T.df, 2, 1), AF.Sign, N, [tk("dp")], [tk("sg0")])
-                act(sl(T.sg, 2, 1), sl(T.sg, 2, 0), AF.Abs, N, [tk("sg0")], [tk("sg1"), tk("cnt")], accum_out=T.cnt[:, c:c + 1])
-            XC = X if NCH == 1 else [X[c]]
-            act(sl(T.bu, 1), T.p0[:, c0:c0 + 16 * N].indirect(T.lst[:, lo:lo + 2 * NB]), AF.Identity, N * GATH,
-                [tk("lst")] + [("p0", a) for a in pieces], [tk("bu")], bias=191.75, scale=0.5)
-            if "bv" in ACTM or ("bv0" in ACTM and c == 0):
-                act(sl(T.bv, 1), T.xs[:, c0:c0 + 16 * N].indirect(T.lst[:, lo:lo + 2 * NB]), AF.Identity, N * GATH, [tk("lst")] + XC, [tk("bv")], scale=0.5)
+                act(ps(T.r2, 4), U["junk"][:], AF.Abs, N + 135, k_("junk"), ["SW"] + k_("cnt"), ["r2"], accum_out=T.cnt[:, c:c + 1])
             else:
-                ts(sl(T.bv, 1), T.xs[:, c0:c0 + 16 * N].indirect(T.lst[:, lo:lo + 2 * NB]), 0.5, None, ALU.mult, None, N * GATH, [tk("lst")] + XC, [tk("bv")])
-            tt(sl(T.bw, 1), sl(T.bu, 1), sl(T.bv, 1), ALU.add, 2 * N, [tk("bu"), tk("bv")], [tk("bw")])
-            t0, t1, e0, e1, q0, q2 = sl(T.tq, 2, 0), sl(T.tq, 2, 1), sl(T.ee, 2, 0), sl(T.ee, 2, 1), sl(T.qq, 2, 0), sl(T.qq, 2, 1)
-            a2, b1, b2 = st(v, 1), st(v, 2), st(v, 3)
-            a2k, bhk = ("a2", v % 2, c), ("bh", v % 2, c)
-            lin("r1", [(ps(T.r1, 0), 1, SH[2], 1, 0), (ps(T.r1, 0), -1, SH[1], 0, 1), (ps(T.r1, 1), 1, SH[2], 1, 0), (ps(T.r1, 1), -1, SH[3], 0, 1)], [shk], ["R1"])
-            tt(sl(T.tq, 2, 0, 2), ps(T.r1, 0, 2), sl(T.fm, 2, 0, 2), ALU.mult, 2 * N, ["R1"] + F, [tk("tq")], ["r1"])
-            lin("r2", [(ps(T.r2, 0, 2), 1, st(v, 5, 2), 1, 0)], [shk], ["R2"])
-            lin("r2", [(ps(T.r2, 0), -1, t0, 0, 0), (ps(T.r2, 0), -1, t1, 0, 0), (ps(T.r2, 1), 1, t1, 0, 1)], [tk("tq")], ["R2"])
-            tt(a2, t0, SH[1], ALU.add, 2 * N, [shk, tk("tq")], [a2k])
-            tt(sl(T.pr, 2, 0, 2), ps(T.r2, 0, 2), st(v, 0, 2), ALU.mult, 2 * N, ["R2", s0k, a2k], [tk("pr")], ["r2"])
-            ts(ps(T.r1, 0, 2), sl(T.pr, 2, 0, 2), col(15), MAGIC, ALU.add, ALU.add, 2 * N, [tk("pr"), "c15"], ["R1"], ["r1"])
-            for e in range(2):
-                tt(sl(T.yy, 2, e), ps(T.r1, e), sl(T.ov, 1), ALU.mult, N, ["R1", tk("ov")], [("yy", c, e)], ["r1"])
-            tt(sl(T.bi, 2, 0, 2), ps(T.r2, 0, 2), sl(T.yy, 2, 0, 2), ALU.add, 2 * N, ["R2", ("yy", c, 0), ("yy", c, 1)], [tk("bi")], ["r2"])
-            ts(sl(T.bn, 2, 0, 2), sl(T.bi, 2, 0, 2), 2047, None, ALU.bitwise_and, None, 2 * N, [tk("bi")], [tk("bn")])
-            cp(st(v, 2, 2), sl(T.bn, 2, 0, 2), 2 * N, [tk("bn")], [bhk])
-            lin("r2", [(ps(T.r2, 0, 2), -1, st(v, 0, 2), 1, 0)], [s0k, a2k], ["R2"])
-            lin("r2", [(ps(T.r2, 0, 2), 1, st(v, 2, 2), 0, 1)], [bhk], ["R2"])
-            for e in range(2):
-                tt(sl(T.ee, 2, e), ps(T.r2, e), sl(T.sw, 1), ALU.mult, N, ["R2", tk("sw")], [("ee", c, e)], ["r2"])
-            E = [("ee", c, 0), ("ee", c, 1)]
-            lin("r1", [(ps(T.r1, 0, 2), 1, st(v, 2, 2), 1, 0), (ps(T.r1, 0), -1, a2, 0, 0), (ps(T.r1, 1), 1, b1, 0, 0),
-                       (ps(T.r1, 1), -1, b2, 0, 0), (ps(T.r1, 1), -1, b2, 0, 0)], [a2k, bhk], ["R1"])
-            lin("r1", [(ps(T.r1, 0), -1, e0, 0, 0), (ps(T.r1, 0), -1, e1, 0, 0), (ps(T.r1, 1), -1, e0, 0, 0), (ps(T.r1, 1), 1, e1, 0, 1)], E, ["R1"])
-            tt(sl(T.qq, 2, 0, 2), ps(T.r1, 0, 2), sl(T.fm, 2, 0, 2), ALU.mult, 2 * N, ["R1"] + F, [tk("qq")], ["r1"])
-            lin("r3", [(ps(T.r3, 0, 4), 1, st(v, 0, 4), 1, 0)], [s0k, a2k, bhk], ["R3"])
-            lin("r3", [(ps(T.r3, 0, 2), 1, sl(T.ee, 2, 0, 2), 0, 0), (ps(T.r3, 2, 2), -1, sl(T.ee, 2, 0, 2), 0, 0)], E, ["R3"])
-            lin("r3", [(ps(T.r3, 1), 1, q0, 0, 0), (ps(T.r3, 2), -1, q0, 0, 0), (ps(T.r3, 2), -1, q2, 0, 0), (ps(T.r3, 3), 1, q2, 0, 1)], [tk("qq")], ["R3"])
-            ob = v * 384 + c * 3 * N
-            cp(T.outb[:, ob:ob + 3 * N], ps(T.r3, 1, 3), 3 * N, ["R3"], [("outb", v, c)], ["r3"])
-            if v < VI - 1:
-                a = ocol(v + 1, c, 0)
-                cp(T.off[:, a:a + N], ps(T.r3, 0), N, ["R3"], [("off", v + 1, c, 0)], ["r3"])
-                cp(st(v + 1, 0), T.off[:, a:a + N], N / 2, [("off", v + 1, c, 0)], [("s0", (v + 1) % 2, c)])
+                act(ps(T.r2, 4), U["junk"][:], AF.Abs, N, k_("junk"), ["SW"], ["r2"])
+            act(ps(T.r2, 5), U["junk"][:], AF.Abs, N, k_("junk"), ["SW2"], ["r2"])
+            if c == 1 and v < VI - 1:
+                n2, n3, n4, n5 = [T.cnt[:, u:u + 1] for u in (2, 3, 4, 5)]
+                act(T.lc[:, 4:6], T.cnt[:, 0:2], AF.Identity, 2, [("cnt", 0), ("cnt", 1)], ["cb"])
+                mm([(T.pk[:, 448:449], T.sel[:], T.lc[:, 4 + u:5 + u], u == 0, u == 1) for u in range(2)], ["sel", "cb"], ["CN"], "pk")
+                act(n2, T.pk[:, 448:449], AF.Identity, 1, ["CN"], ["n2"], ["pk"], bias=-7.75)
+                act(n3, n2, AF.Identity, 1, ["n2"], ["n3"], bias=M16)
+                act(n4, n3, AF.Identity, 1, ["n3"], ["n4"], bias=M16, scale=-1.0)
+                act(n5, n4, AF.Identity, 1, ["n4", "n2"], ["n5"], bias=n2)
+                act(T.thf[:, 0:1], n5, AF.Identity, 1, ["n5", "th3"], ["thr"], bias=T.thf[:, 1:2])
+            lin("r2", [(ps(T.r2, 2, 2), I16, S23)], IHS + ["i16+"], ["R2"], True)
+            ts(ps(U["fm"], 0), U["tf"][:], 2048.0, None, ALU.is_lt, None, N, k_("tf"), k_("f0"))
+            ts(ps(U["fm"], 1), U["tf"][:], 4096.0, None, ALU.is_ge, None, N, k_("tf"), k_("f2"))
+            ts(U["xf"][:], U["tf"][:], 2047, None, ALU.bitwise_and, None, N, k_("tf"), k_("xf"))
+            tt(U["ov"][:], U["xf"][:], ps(T.r1, 4), ALU.is_gt, N, k_("xf") + ["Y"], k_("ov"), ["r1"])
+            FM = k_("f0", "f2")
+            scan(U["run"][:], T.keep[:], U["rt"][:], ALU.mult, ALU.add, k_("rt") + ["keep"], k_("run"))
+            lin("pl", [(T.pl[:, 0:4], IB, T.lc[:, 0:4])], ["ib+", "lc"], ["L"], True)
+            lin("pl", [(T.pl[:, 2 * jh:2 * jh + 2], T.pm[:, 128 * (2 * jh + h):128 * (2 * jh + h) + 128], U["run"][:, 16 * h + 15:N:32])
+                       for jh in range(2) for h in range(2)], [("pm", j) for j in range(4)] + k_("run"), ["L"], False, True)
+            lc, xc = T.lst[:, 4 * c:4 * c + 4], T.xs[:, LK * c:LK * c + LK]
+            cp(lc, T.pl[:, 0:4], 4, ["L"], k_("lst"), ["pl"])
+            if c in CFG["bwv"]:
+                act(U["bu"][:], ga(0, 0, LK).indirect(lc), AF.Identity, N * GATH, k_("lst") + gt(0, 0, LK), k_("bu"), bias=191.75, scale=-0.5)
+                act(U["bv"][:], xc.indirect(lc), AF.Identity, N * GATH, k_("lst") + [X[c]], k_("bv"), scale=0.5)
+                tt(U["bw"][:], U["bu"][:], U["bv"][:], ALU.add, 2 * N, k_("bu", "bv"), k_("bw"))
             else:
-                cp(T.ysf[:, c * N:(c + 1) * N], ps(T.r3, 0), N, ["R3"], [("ys", c, 0)], ["r3"])
-            trs = []
+                act(ps(U["bb"], 0), ga(0, 0, LK).indirect(lc), AF.Identity, N * GATH, k_("lst") + gt(0, 0, LK), k_("bu"), scale=-1.0)
+                act(ps(U["bb"], 1), xc.indirect(lc), AF.Identity, N * GATH, k_("lst") + [X[c]], k_("bv"))
+            for u in range(2 * c):
+                if u not in CFG["bwv"]:
+                    bk = "pd%d" % u
+                    lin(bk, [(ps(T[bk], 0), IB, ps(T["bb%d" % u], e)) for e in range(2)], ["ib+", ("bu", u), ("bv", u)], [bk], True, True)
+                    act(T["bw%d" % u][:], ps(T[bk], 0), AF.Identity, N, [bk], [("bw", u)], [bk], bias=191.75, scale=0.5)
+                tt(T.xs[:, LK * u:LK * u + LK].indirect(T.lst[:, 4 * u:4 * u + 4]), T["bw%d" % u][:], T.m192[:], ALU.add, N * CFG["scat"],
+                   [("lst", u), ("bw", u), "m192"], [X[u]])
+            t0, t1, d1, d2, e1, e2, q0, q2 = [ps(U[b], j) for b in ("tq", "dd", "ee", "qq") for j in range(2)]
+            zero("r3", 0, 256, ["R3"])
+            lin("r3", [(ps(T.r3, j), IH, (S0, S1)[j % 2]) for j in range(4)], IHS, ["R3"])
+            tt(U["tq"][:], ps(T.r1, 0, 2), U["fm"][:], ALU.mult, 128, ["R1"] + FM, k_("tq"), ["r1"])
+            TQ = IHS + k_("tq")
+            mm([(ps(T.pl, 1), IH, S0, True, True), (ps(T.pl, 2), IH, S1, True, False)], IHS, ["RA"], "pl")
+            lin("pl", [(ps(T.pl, 2), IH, t0)], TQ, ["RA"], False, True)
+            lin("r2", [(ps(T.r2, 2), N16, t0), (ps(T.r2, 2), N16, t1), (ps(T.r2, 3), I16, t1), (ps(T.r2, 2), T.dk[:], U["ov"][:]), (ps(T.r2, 3), T.dk[:], U["ov"][:])],
+                TQ + ["i16+", "i16-", "dk"] + k_("ov"), ["R2"], False, True)
+            lin("r2", [(ps(T.r2, 0, 2), IH, S23), (ps(T.r2, 0), NH, t0), (ps(T.r2, 0), NH, t1), (ps(T.r2, 1), IH, t1)], TQ, ["R2"], True, True)
+            lin("r3", [(ps(T.r3, 1), IH, t0), (ps(T.r3, 3), IH, t0)], TQ, ["R3"])
+            zero("r1", 128, 128, ["R1"])
+            lin("r1", [(ps(T.r1, 2 + e), m, x) for e in range(2) for m, x in ((IH, S0), (NH, S1), (NH, t0))], TQ, ["R1"])
+            for e in range(2):
+                tt(ps(U["ao"], e), ps(T.pl, 1 + e), U["ov"][:], ALU.mult, N, ["RA"] + k_("ov"), k_("ao%d" % e), ["pl"])
+            tt(U["pr"][:], ps(T.r2, 0, 2), U["ao"][:], ALU.mult, 128, ["R2"] + k_("ao0", "ao1"), k_("pr"), ["r2"])
+            tt(U["zi"][:], ps(T.r2, 2, 2), U["pr"][:], ALU.add, 128, ["R2"] + k_("pr"), k_("zi"), ["r2"])
+            ts(U["bn"][:], U["zi"][:], 4, 2047, ALU.arith_shift_right, ALU.bitwise_and, 128, k_("zi"), k_("bn"))
+            tt(U["dd"][:], U["bn"][:], ps(T.pl, 1, 2), ALU.subtract, 128, k_("bn") + ["RA"], k_("dd"), ["pl"])
+            lin("r1", [(ps(T.r1, 2), IH, d1), (ps(T.r1, 3), IH, d1), (ps(T.r1, 3), NH, d2)], IHS + k_("dd"), ["R1"])
+            lin("r3", [(ps(T.r3, 2, 2), IH, U["dd"][:])], IHS + k_("dd"), ["R3"])
+            tt(U["ee"][:], ps(T.r2, 4, 2), U["dd"][:], ALU.mult, 128, ["SW", "SW2"] + k_("dd"), k_("ee"), ["r2"])
+            E = IHS + k_("ee")
+            lin("r1", [(ps(T.r1, 2), NH, e1), (ps(T.r1, 2), NH, e2), (ps(T.r1, 3), NH, e1), (ps(T.r1, 3), IH, e2)], E, ["R1"], False, True)
+            lin("r3", [(ps(T.r3, 0, 2), IH, U["ee"][:]), (ps(T.r3, 2, 2), NH, U["ee"][:])], E, ["R3"])
+            tt(U["qq"][:], ps(T.r1, 2, 2), U["fm"][:], ALU.mult, 128, ["R1"] + FM, k_("qq"), ["r1"])
+            lin("r3", [(ps(T.r3, 1), IH, q0), (ps(T.r3, 2), NH, q0), (ps(T.r3, 2), NH, q2), (ps(T.r3, 3), IH, q2)], IHS + k_("qq"), ["R3"], False, True)
+            ob = ocol(v + 1, c, 0)
+            cp(T.off[:, ob:ob + 4 * N], ps(T.r3, 0, 4), 4 * N, ["R3"], [("off", v + 1, c, 0)], ["r3"])
+            trs = [[], []]
             for s in (1, 2, 3):
-                hop, rel, mask = rt[(rank, s)]
+                hop, rel, mask, call = rt[(rank, s)]
                 rid, pid = topo.addr(hop, core)
                 a = ocol(v + 1, c, s)
-                trs.append(RemoteDMATransfer(dst_ids=[DstId(rid=rid, pnc=pid)], dma_engine_mask=mask, remote_sem=T.sem["a%d_%d_%d" % (v, c, s)],
-                                             src=T.outb[:, ob + (s - 1) * N:ob + s * N], dst=T.off[:, a:a + N]))
+                trs[call].append(RemoteDMATransfer(dst_ids=[DstId(rid=rid, pnc=pid)], dma_engine_mask=mask, remote_sem=T.sem["a%d_%d_%d" % (v, c, s)],
+                                                   src=T.off[:, ob + s * N:ob + (s + 1) * N], dst=T.off[:, a:a + N]))
                 sent[0] += bits(mask)
-            snd = add("G", lambda trs=trs: g.remote_dma_fused(trs, local_sem=T.sem.sent), 1000.0, [("outb", v, c)], (), sem=("", 0))
+            snd = add("G", lambda trs=trs: [g.remote_dma_fused(t, local_sem=T.sem.sent) for t in trs], 1000.0, [("off", v + 1, c, 0)], (), sem=("", 0, 0))
             for s in (1, 2, 3):
                 r0 = (rank - STEP[s]) % NR
-                hop, rel, mask = rt[(r0, s)]
+                hop, rel, mask, call = rt[(r0, s)]
                 cntv = bits(mask) if rel is None else bits(topo.mask(rel, core))
-                add("N", None, CFG["net"], (), [("off", v + 1, c, s)], sem=("a%d_%d_%d" % (v, c, s), cntv), after=[snd])
-            if v == VI - 1:
-                for s in (1, 2, 3):
-                    a = ocol(VI, c, s)
-                    cp(T.ysf[:, s * TT + c * N:s * TT + (c + 1) * N], T.off[:, a:a + N], N, [("off", VI, c, s)], [("ys", c, s)])
-        for c in range(NCH):
-            tt(T.xs[:, c * 16 * N:(c + 1) * 16 * N].indirect(T.lst[:, c * 2 * NB:(c + 1) * 2 * NB]), T.bw[:, c * N:(c + 1) * N], T.m192[:], ALU.add,
-               N * CFG["scat"], [("lst", c), ("bw", c), "m192"], X if NCH == 1 else [X[c]])
-        if v < VI - 1:
-            CN = [("cnt", c) for c in range(NCH)]
-            if NCH == 1:
-                cp(T.ai[:, 0:1], T.cnt[:, 0:1], 1, CN, ["ai0"])
+                add("N", None, CFG["net"][s] + (CFG["once"] if v == c == 0 else 0.0), (), [("off", v + 1, c, s)], sem=("a%d_%d_%d" % (v, c, s), cntv, 0), after=[snd])
+            if v < VI - 1:
+                pass
             else:
-                tt(T.ai[:, 0:1], T.cnt[:, 0:1], T.cnt[:, 1:2], ALU.add, 1, CN, ["ai0"])
-            ts(T.ai[:, 1:2], T.ai[:, 0:1], 31, None, ALU.bitwise_and, None, 1, ["ai0"], ["ai1"])
-            tt(T.thr[:, 0:1], T.ai[:, 1:2], T.thi[:, 0:1], ALU.add, 1, ["ai1", "thi"], ["thr"])
-    dma("A", T.yx[:], T.xs[:], "st0", X, ())
-    dma("S", T.ys[:], T.ysf[:], "st1", [("ys", c, s) for c in range(NCH) for s in range(4)], ())
-    return ops, sent[0]
+                if c == 1:
+                    stores.append(dma("S", T.yx[:], T.xs[:], "st", 0, X, ()))
+                for s in (0,) + CFG["role"]:
+                    a, y = ocol(VI, c, s), TT * s + N * c
+                    cp(T.ysf[:, y:y + N], T.off[:, a:a + N], N, [("off", VI, c, s)], [("ys", c, s)])
+                    stores.append(dma("SA"[s % 2], T.ys[:, y:y + N], T.ysf[:, y:y + N], "st", 0, [("ys", c, s)], ()))
+    return ops, sent[0], 16 * len(stores)
 
 
-def emit(g, T, ops, order, sent):
+def emit(g, T, ops, order, sent, stored):
     queue = {"V": g.vector, "A": g.scalar, "P": g.tensor, "G": g, "S": g.sync}
     csem = {"V": "cv", "A": "ca", "P": "cp", "G": "cg"}
     mark, total = {}, {}
@@ -483,7 +641,7 @@ def emit(g, T, ops, order, sent):
         for i in order[q]:
             if ops[i]["sem"] is None:
                 k += 1
-                mark[i] = (csem[q], k)
+                mark[i] = (csem[q], k, 1)
             else:
                 mark[i] = ops[i]["sem"]
         if k:
@@ -495,42 +653,46 @@ def emit(g, T, ops, order, sent):
             for d in ops[i]["deps"]:
                 if q == "P" and ops[d]["q"] == "P":
                     continue
-                s, val = mark[d]
+                s, val, inc = mark[d]
                 need[s] = max(need.get(s, 0), val)
             for s in need:
                 if need[s] > seen.get(s, 0):
                     queue[q].wait_ge(T.sem[s], need[s])
                     seen[s] = need[s]
             ins = ops[i]["fn"]()
-            s, val = mark[i]
+            s, val, inc = mark[i]
             if s:
-                ins.then_inc(T.sem[s], 1 if ops[i]["sem"] is None else val)
+                ins.then_inc(T.sem[s], inc)
     for s in total:
         g.wait_ge(T.sem[s], total[s])
     g.wait_ge(T.sem.sent, sent)
-    g.wait_ge(T.sem.st0, 16)
-    g.wait_ge(T.sem.st1, 16)
+    g.wait_ge(T.sem.st, stored)
 
 
 def rank_program(g, core, T, topo):
     rt = routes(T, topo)
     rank = T.rank_of(core)
     if rank is not None:
-        ops, sent = build(g, core, T, topo, rank, rt)
+        ops, sent, stored = build(g, core, T, topo, rank, rt)
         if "order" not in _PLAN:
-            _PLAN["order"], _PLAN["end"] = schedule(ops)
+            cases, mid = [(ops, CFG["ls"], CFG["lx"])], dict(CFG)
+            for case in CFG["cases"]:
+                CFG.update(case)
+                cases.append((build(g, core, T, topo, rank, rt)[0], CFG["ls"], CFG["lx"]))
+                CFG.update(mid)
+            _PLAN["order"], _PLAN["end"] = min([schedule(cases, seed) for seed in CFG["seeds"]], key=lambda plan: plan[1])
             _PLAN["ops"] = ops
-        emit(g, T, ops, _PLAN["order"], sent)
+        emit(g, T, ops, _PLAN["order"], sent, stored)
         return
-    for (r, s), (hop, rel, mask) in rt.items():
+    for (r, s), (hop, rel, mask, call) in rt.items():
         if rel == core:
             dst = T.cores[(r + STEP[s]) % NR]
             rid, pid = topo.addr(dst, core)
             m2 = topo.mask(core, dst)
             for v in range(VI):
-                for c in range(NCH):
+                for c in range(2):
                     a = ocol(v + 1, c, s)
                     sem = T.sem["a%d_%d_%d" % (v, c, s)]
                     g.wait_ge(sem, bits(mask))
                     g.remote_dma(T.off[:, a:a + N], T.off[:, a:a + N], sem, T.sem.sent, pid, rid, m2)
-            g.wait_ge(T.sem.sent, bits(m2) * VI * NCH)
+            g.wait_ge(T.sem.sent, bits(m2) * VI * 2)

from concourse.bass import DstId, RemoteDMATransfer
from concourse.mybir import AluOpType as ALU, ActivationFunctionType as AF

NR, VI, TT, WX = 8, 6, 128, 2048
STEP = (0, 1, 3, 4)
N = 64
LK = 16 * N
BLK = 7 * N
OFFK = 12582912.0
M2048 = 25769803776.0
M16 = 201326592.0
H, B, F, I = "float16", "bfloat16", "float32", "int32"
S_, P_ = "sbuf", "psum"

OWN = {"sh": (4, H), "wt": (6, H), "ch": (3, H), "m1": (2, F), "mk": (2, I), "tk": (2, I), "dt": (1, F), "dq": (1, F), "dv": (1, F),
       "uu": (1, F), "rt": (1, F), "run": (1, B), "tf": (1, I), "xf": (1, I), "fm": (2, H), "ov": (1, H), "junk": (1, F), "tq": (2, H),
       "ao": (2, F), "pr": (2, F), "zi": (2, I), "bn": (2, I), "dd": (2, H), "ee": (2, H), "qq": (2, H), "bu": (1, F), "bv": (1, F),
       "bw": (1, B), "bb": (2, B), "wd": (7, H), "ga": (64, B), "ab": (96, B)}
SCRATCH = {
    "xs": (S_, [128, WX], B), "homi": (S_, [128, 512], I), "thi": (S_, [128, 8], I), "thf": (S_, [128, 8], F),
    "off": (S_, [128, (VI + 1) * 2 * BLK], "uint16"), "ysf": (S_, [128, 512], F), "pi": (S_, [128, 8], I), "cf": (S_, [128, 24], F),
    "dj": (S_, [128, 128], B), "jg": (S_, [128, 128], B), "j8": (S_, [128, 32], B), "jb": (S_, [128, N], B),
    "wm": (S_, [128, 384], B), "em": (S_, [128, N], H), "lci": (S_, [128, 8], F), "lc": (S_, [128, 8], B),
    "ib": (S_, [128, 256], B), "ih": (S_, [128, 256], H), "i16": (S_, [128, 256], H), "dk": (S_, [128, 128], H),
    "pm": (S_, [128, 512], B), "zm": (S_, [128, 512], H), "jw": (S_, [128, 144], B), "wb": (S_, [128, 432], B), "gm": (S_, [128, 64], B), "sel": (S_, [128, 128], B),
    "ka": (S_, [128, 128], B), "kb": (S_, [128, 256], B), "zb": (S_, [128, 384], B), "m192": (S_, [128, N], B),
    "one": (S_, [128, N], F), "kp3": (S_, [128, N], F), "keep": (S_, [128, N], F), "cnt": (S_, [128, 8], F), "lst": (S_, [128, 8], "uint16"),
}
SCRATCH.update({b: (P_, [128, 512], F) for b in ("pd0", "pd1", "pc", "pk", "pl", "r1", "r2", "r3")})
SCRATCH.update({nm + str(c): (S_, [128, OWN[nm][0] * N], OWN[nm][1]) for nm in OWN for c in range(2)})
SEMAPHORES = (["cv", "ca", "cp", "cg", "sent", "lx0", "lx1", "lh0", "lh1", "lt", "st"]
              + ["a%d_%d_%d" % (v, c, s) for v in range(VI) for c in range(2) for s in (1, 2, 3)] + ["d%d" % j for j in range(24)])

CFG = {"cyc": 0.9, "pe": 0.5, "gath": 1.56, "scat": 3.8, "net": (0.0, 4800.0, 3600.0, 5600.0), "ov": 50.0, "oa": 65.0, "ls": 140.0, "lx": 210.0,
       "lam": 4000.0, "delta": 2000.0, "theta": 0.2, "tol": 800.0, "passes": 400, "seeds": (1,), "span": 6, "swaps": 11000, "tol3": 300.0,
       "cases": ({"cyc": 1.2, "gath": 2.0, "ls": 180.0, "lx": 270.0},
                 {"cyc": 0.87, "gath": 1.2, "ls": 110.0, "lx": 220.0, "net": (0.0, 5800.0, 4600.0, 6600.0)}),
       "dma": (), "pd": (512, 512), "dlat": 4000.0,
       "once": 5000.0, "wait1": 15000.0,
       "pv": ((512, 512), (512, 512), (512, 512)),
       "pa": (256, 768),
       "pb": 512,
       "rs": 4,
       "role": (2, 1, 3),
       "pairs": (((1, 2), (2, 3), (1, 3)), ((1, 2), (2, 3), (1, 3))),
       "relu": ((1, 3),),
       "plain": (), "mov": (), "dei": (), "dqa": (), "bwv": (1,)}
_PLAN = {}


def routes(T, topo):
    out = {}
    for r in range(NR):
        src = T.cores[r]
        used, hops = [], []
        for s in CFG["role"]:
            dst = T.cores[(r + STEP[s]) % NR]
            if topo.may_write(src, dst):
                hops.append((s, dst, None))
            else:
                cand = [c for c in topo.cores_of(src) if c != src and c not in used and topo.may_write(c, dst)]
                cand.sort(key=lambda c: (topo.die(c) != topo.die(src), c))
                used.append(cand[0])
                hops.append((s, cand[0], cand[0]))
        taken = []
        for s, hop, rel in hops:
            free = [e for e in topo.engines(src, hop) if e not in taken]
            if len(taken) < 16 and len(free) >= 8:
                taken += free[:8]
                out[(r, s)] = (hop, rel, sum(1 << e for e in free[:8]), 0)
            else:
                out[(r, s)] = (hop, rel, topo.mask(src, hop), 1)
    return out


def bits(m):
    return bin(m).count("1")


def ocol(v, c, s):
    return (v * 2 + c) * BLK + (s - 1 if s else 3) * N


def schedule(cases, start):
    ops = cases[0][0]
    n = len(ops)
    pre = [[(i, ops[i]["hold"] if ops[i]["q"] == o["q"] == "P" else ops[i]["cost"] + (CFG["ls"] if ops[i]["q"] == o["q"] else CFG["lx"]))
            for i in o["deps"]] for o in ops]
    succ = [[] for _ in range(n)]
    for j in range(n):
        for i, l in pre[j]:
            succ[i].append((j, l))
    tail = [0.0] * n
    for i in range(n - 1, -1, -1):
        tail[i] = max([l + tail[j] for j, l in succ[i]] + [ops[i]["cost"]])
    first = {}
    for i, o in enumerate(ops):
        first.setdefault(o["blk"], i)
    nt = first[6] - first[4]
    q_of, hold, cost, blk = [o["q"] for o in ops], [o["hold"] for o in ops], [o["cost"] for o in ops], [o["blk"] for o in ops]
    place = [(-1 if blk[i] < 0 else min(i - first[blk[i] // 2 * 2], nt - 1)) for i in range(n)]
    base = [tail[i] - CFG["lam"] * (max(blk[i], 0) // 2) - CFG["delta"] * (max(blk[i], 0) % 2) - CFG["wait1"] * (blk[i] == 1) for i in range(n)]
    seed = [start]

    def rnd(k):
        seed[0] = (seed[0] * 1103515245 + 12345) % 2147483648
        return (seed[0] >> 8) % k

    def listed(off, m):
        pr = [base[i] + (off[place[i]] if place[i] >= 0 else 0.0) for i in range(m)]
        left = [len(pre[i]) for i in range(m)]
        ready, at, free, pool = [0.0] * m, [0.0] * m, {}, {}
        for i in range(m):
            free[q_of[i]] = 0.0
            pool.setdefault(q_of[i], [])
            if left[i] == 0:
                pool[q_of[i]].append(i)
        done, end = 0, 0.0
        while done < m:
            t, q = 1e18, None
            for u in pool:
                if pool[u]:
                    w = max(free[u], min([ready[i] for i in pool[u]]))
                    if w < t:
                        t, q = w, u
            p = pool[q]
            i = max([j for j in p if ready[j] <= t + 1.0], key=lambda j: pr[j])
            if q != "N":
                soon = [ready[j] for j in p if pr[j] > pr[i] and ready[j] <= t + CFG["theta"] * hold[i]]
                if soon:
                    free[q] = min(soon)
                    continue
                free[q] = t + hold[i]
            p.remove(i)
            at[i] = t
            end = max(end, t + cost[i])
            done += 1
            for j, l in succ[i]:
                if j < m:
                    ready[j] = max(ready[j], t + l)
                    left[j] -= 1
                    if left[j] == 0:
                        pool[q_of[j]].append(j)
        return at, end
    m = first[CFG["span"]]
    off = [0.0] * nt
    end = listed(off, m)[1]
    best = (off, end)
    for it in range(CFG["passes"]):
        b = list(off)
        a, w = rnd(nt), (1, 1, 2, 4, 8, 16)[rnd(6)]
        d = (-1, 1)[rnd(2)] * (150, 400, 1000, 2500, 6000)[rnd(5)]
        for u in range(a, min(nt, a + w)):
            b[u] += d
        e = listed(b, m)[1]
        if e <= end + CFG["tol"] * (1 - it / CFG["passes"]) * rnd(100) / 100.0:
            off, end = b, e
            if end < best[1]:
                best = (off, end)
    at0, end0 = listed(best[0], n)

    sends = [at0[i] for i in range(first[0], n) if q_of[i] == "G" and not ops[i]["sem"][0]]
    per = sends[6] - sends[4]
    slot, shift, key = [0] * n, [0.0] * n, [at0[i] - 2 * per for i in range(first[4], first[6])]
    for i in range(n):
        v = blk[i] // 2
        if 1 < v < VI - 1:
            slot[i], shift[i] = i - first[2 * v], v * per
            continue
        slot[i] = len(key)
        if v < 2:
            key.append(at0[i] if ops[i]["sem"] is None or v >= 0 else i - 1e3)
            continue
        if i == first[blk[i]]:
            like = first[4 + blk[i] % 2]
        same = [u for u in range(like, min(like + 12, first[5 + blk[i] % 2])) if q_of[u] == q_of[i] and cost[u] == cost[i]]
        if same:
            key.append(max([key[same[0] - first[4]] + v * per] + [key[slot[d]] + shift[d] + 0.01 for d, l in pre[i]]))
            like = same[0] + 1
        else:
            key.append(max([0.0] + [key[slot[d]] + shift[d] + l for d, l in pre[i]]))
    byq = {}
    for i in range(n):
        if q_of[i] != "N":
            byq.setdefault(q_of[i], []).append(i)

    pres = [[[(i, a[i]["hold"] if q_of[i] == q_of[j] == "P" else a[i]["cost"] + (ls if q_of[i] == q_of[j] else lx)) for i in ops[j]["deps"]]
             for j in range(n)] for a, ls, lx in cases]
    holds, costs = [[o["hold"] for o in a] for a, ls, lx in cases], [[o["cost"] for o in a] for a, ls, lx in cases]
    ends = [i for i in range(n) if not succ[i]]

    def ordered(key, pick):
        nxt, prv, left = [-1] * n, [-1] * n, [len(p) for p in pre]
        for q in byq:
            o = sorted(byq[q], key=lambda i: key[slot[i]] + shift[i])
            for a, b in zip(o, o[1:]):
                nxt[a], prv[b] = b, a
                left[b] += 1
        seq = [i for i in range(n) if left[i] == 0]
        for i in seq:
            for j, l in succ[i]:
                left[j] -= 1
                if left[j] == 0:
                    seq.append(j)
            j = nxt[i]
            if j >= 0:
                left[j] -= 1
                if left[j] == 0:
                    seq.append(j)
        if len(seq) < n:
            return None, 1e18, []
        total, held = 0.0, []
        for u in range(len(cases)):
            pu, hu, at = pres[u], holds[u], [0.0] * n
            for i in seq:
                j = prv[i]
                t = at[j] + hu[j] if j >= 0 else 0.0
                for d, l in pu[i]:
                    if at[d] + l > t:
                        t = at[d] + l
                at[i] = t
            fin = max(ends, key=lambda i: at[i] + costs[u][i])
            total += at[fin] + costs[u][fin]
            if u == 0:
                times = at
            while u == pick and at[fin] > 0.0:
                j = prv[fin]
                if j >= 0 and at[j] + hu[j] == at[fin]:
                    held.append((fin, j))
                    fin = j
                else:
                    fin = max(pu[fin], key=lambda e: at[e[0]] + e[1])[0]
        return times, total / len(cases), held
    at, end, held = ordered(key, 0)
    best = (at0, 1e18, at0)
    for it in range(CFG["swaps"] if held else 0):
        i, j = held[rnd(len(held))]
        b = list(key)
        far = (0.01, 0.01, 200.0, 1000.0)[rnd(4)]
        if rnd(2):
            b[slot[i]] = key[slot[j]] + shift[j] - far - shift[i]
        else:
            b[slot[j]] = key[slot[i]] + shift[i] + far - shift[j]
        at, e, held2 = ordered(b, rnd(len(cases)))
        if e <= end + CFG["tol3"] * (1 - it / CFG["swaps"]) * rnd(100) / 100.0:
            key, end, held = b, e, held2
            if end < best[1]:
                best = ([key[slot[u]] + shift[u] for u in range(n)], end, at)
    order = {}
    for i in sorted(range(n), key=lambda i: (best[0][i], i)):
        order.setdefault(q_of[i], []).append(i)
        ops[i]["t"] = best[2][i]
    return order, best[1]


def build(g, core, T, topo, rank, rt):
    ops, lastw, readers, lock = [], {}, {}, {}
    blk = [-1]
    V, A, PE = g.vector, g.scalar, g.tensor
    CYC, GATH = CFG["cyc"], CFG["gath"]

    def add(q, fn, cost, r=(), w=(), bank=(), sem=None, hold=None, after=()):
        i = len(ops)
        deps = set(after)
        for t in r:
            deps.update(lastw.get(t, ()))
        for t in w:
            deps.update(lastw.get(t, ()))
            deps.update(readers.get(t, ()))
        for b in bank:
            users = lock.setdefault(b, [])
            if users and ops[users[-1]]["q"] != q:
                lock[(b, "pre")] = list(users)
                lock[b] = users = []
            deps.update(lock.get((b, "pre"), ()))
            users.append(i)
        for t in r:
            readers.setdefault(t, []).append(i)
        for t in w:
            lastw[t] = [i]
            readers[t] = []
        deps.discard(i)
        ops.append({"q": q, "fn": fn, "cost": cost, "deps": sorted(deps), "sem": sem, "hold": cost if hold is None else hold, "blk": blk[0]})
        return i

    def vc(cyc):
        return CFG["ov"] + max(64.0, cyc) * CYC

    def ts(out, in0, s1, s2, o0, o1, cyc, r, w, bank=()):
        if o1 is None:
            return add("V", lambda: V.tensor_scalar(out, in0, s1, None, o0), vc(cyc), r, w, bank)
        return add("V", lambda: V.tensor_scalar(out, in0, s1, s2, o0, o1), vc(cyc), r, w, bank)

    def tt(out, in0, in1, op, cyc, r, w, bank=()):
        return add("V", lambda: V.tensor_tensor(out, in0, in1, op), vc(cyc), r, w, bank)

    def cp(out, in_, cyc, r, w, bank=()):
        return add("V", lambda: V.tensor_copy(out, in_), vc(cyc), r, w, bank)

    def scan(out, d0, d1, o0, o1, r, w):
        return add("V", lambda: V.tensor_tensor_scan(out, d0, d1, 0.0, o0, o1), vc(N), r, w)

    def turn(out, in_, r, w, bank=()):
        return add("V", lambda: V.transpose(out, in_), vc(N), r, w, bank)

    def act(out, in_, f, cyc, r, w, bank=(), **kw):
        return add("A", lambda: A.activation(out, in_, f, **kw), CFG["oa"] + max(64.0, cyc) * CYC, r, w, bank)

    def mm(lst, r, w, bank, wide=1):
        def fn():
            ins = None
            for (o, l, x, st, sp) in lst:
                ins = PE.matmul(o, l, x, st, sp)
            return ins
        hold = sum(max(64, m[2].shape[1]) * CFG["pe"] * wide for m in lst)
        return add("P", fn, hold + 50.0, r, w, [bank], hold=hold)

    def lin(bank, terms, r, w, start=False, stop=False):
        return mm([(o, m, x, start and j == 0, stop and j == len(terms) - 1) for j, (o, m, x) in enumerate(terms)], r, w, bank)

    def zero(bank, a, n, w):
        return lin(bank, [(T[bank][:, a:a + n], T.zb[:, 0:128], T.zb[:, 0:n])], ["zb"], w, True)

    def dma(q, out, in_, sem, total, r, w):
        e = g.sync if q == "S" else g.scalar
        return add(q, lambda: e.dma_start(out, in_), 2500.0, r, w, sem=(sem, total, 16), hold=60.0)

    def iota(out, pat, base, mult, cyc, w, small=True):
        if small:
            return add("G", lambda: g.iota(out, pat, base, mult, allow_small_or_imprecise_dtypes=True), 130.0 + 2 * cyc, (), w)
        return add("G", lambda: g.iota(out, pat, base, mult), 130.0 + 2 * cyc, (), w)

    def col(j):
        return T.cf[:, j:j + 1]

    def ps(buf, j, m=1):
        return buf[:, j * N:(j + m) * N]

    h0 = dma("S", T.homi[:, 0:TT], T.hom[:, 0:TT], "lh0", 16, (), [("homi", 0)])
    xl = [dma("AS"[c], T.xs[:, LK * c:LK * c + LK], T.x[:, LK * c:LK * c + LK], "lx%d" % c, 16, (), [("x", c)]) for c in range(2)]
    dma("A", T.homi[:, TT:4 * TT], T.hom[:, TT:4 * TT], "lh1", 16, (), [("homi", s) for s in (1, 2, 3)])
    dma("S", T.thi[:, 0:1], T.th[:], "lt", 16, (), ["thi"])
    X, xw = [("x", 0), ("x", 1)], T.xs[:, 0:WX]
    for c in range(2):
        for s in (0,) + CFG["role"]:
            a = ocol(0, c, s)
            cp(T.off[:, a:a + N], T.homi[:, TT * s + N * c:TT * s + N * c + N], N, [("homi", s)], [("off", 0, c, s)])
    iota(T.dj[:], [[1, 128]], 0, -1, 128, ["dj"])
    iota(T.pi[:, 0:1], [[0, 1]], 0, 1, 1, ["pi0"], False)
    iota(T.zb[:], [[0, 384]], 0, 0, 384, ["zb"])
    iota(T.j8[:], [[0, 2], [1, 8], [0, 2]], 0, 0, 32, ["j8"])
    iota(T.wm[:], [[0, 24], [1, 2], [0, 8]], 0, 0, 384, ["jw"])
    iota(T.jb[:], [[1, N]], 0, 0, N, ["jb"])
    iota(T.jg[:], [[1, 8], [0, 16]], 0, 0, 128, ["jg"])
    iota(T.ka[0:2, :], [[0, 128]], int(OFFK), 1024 - int(OFFK), 128, ["ka"])
    for p in (1, 2):
        iota(T.kb[0:2, 128 * p - 128:128 * p], [[0, 128]], 1, 2 * p, 128, [("kb", p)])
    iota(T.one[:], [[0, N]], 1, 0, N, ["one"])
    for buf, nm, lim in ((T.kp3, "kp3", 3), (T.keep, "keep", 1)):
        add("G", lambda buf=buf, lim=lim: g.affine_select(buf[:], T.one[:], [[0, 4], [1, 16]], ALU.is_ge, 0.0, -lim, 0), 170.0 + 2 * N, ["one"], [nm])
    iota(T.lci[:, 0:4], [[256, 2], [512, 2]], 16, 0, 4, ["lci"])
    iota(T.m192[:], [[0, N]], -192, 0, N, ["m192"])
    for j, (sh, msk) in enumerate(((4, 7), (0, 15), (0, 16), (1, 63), (0, 1))):
        ts(T.pi[:, j + 1:j + 2], T.pi[:, 0:1], sh, msk, ALU.arith_shift_right, ALU.bitwise_and, 1, ["pi0"], ["pi%d" % (j + 1)])
    cp(T.cf[:, 0:6], T.pi[:, 0:6], 8, ["pi%d" % j for j in range(6)], ["c0"])
    cP, cG, cK, cH, cT, cO = [col(j) for j in range(6)]
    for buf, nm, val in ((T.ib, "ib", 1.0), (T.ih, "ih", 1.0), (T.i16, "i16", 16.0)):
        ts(buf[:, 0:128], T.dj[:], 0.0, val, ALU.is_equal, ALU.mult, 64, ["dj"], [nm + "+"])
        ts(buf[:, 128:256], T.dj[:], 0.0, -val, ALU.is_equal, ALU.mult, 64, ["dj"], [nm + "-"])
    IB, NB, IH, NH, I16, N16 = T.ib[:, 0:128], T.ib[:, 128:256], T.ih[:, 0:128], T.ih[:, 128:256], T.i16[:, 0:128], T.i16[:, 128:256]
    for a, b, val in ((0, 32, -0.5), (32, 48, 1.0), (48, 64, 0.5)):
        ts(T.gm[:, a:b], T.j8[:, 0:b - a], cG, val, ALU.is_equal, ALU.mult, 16, ["j8", "c0"], [("gm", a)])
    GM = [("gm", a) for a in (0, 32, 48)]
    ts(T.em[:], T.jb[:], cT, None, ALU.is_equal, None, 64, ["jb", "c0"], ["em"])
    ts(T.wm[:], T.wm[:], cO, None, ALU.is_equal, None, 192, ["jw", "c0"], ["wm"])
    for j, (lim, op) in enumerate(((3.0, ALU.is_lt), (13.0, ALU.is_ge))):
        ts(col(6 + j), cK, lim, 8192.0, op, ALU.mult, 1, ["c0"], [("c", 6 + j)])
        ts(T.zm[:, 128 * j:128 * j + 128], T.jg[:], cG, col(6 + j), ALU.is_equal, ALU.mult, 64, ["jg", "c0", ("c", 6 + j)], [("zm", j)])
    act(col(8), col(7), AF.Identity, 1, [("c", 7)], [("c", 8)], bias=M2048, scale=4.0)
    if CFG["mov"]:
        ts(T.zm[:, 256:512], T.zm[:, 0:256], -1.0, None, ALU.mult, None, 128, [("zm", 0), ("zm", 1)], [("zm", 2), ("zm", 3)])
        iota(T.jw[:], [[1, 144]], -15, 0, 144, ["jv"])
        act(col(10), cG, AF.Identity, 1, ["c0"], [("c", 10)], scale=16.0)
        for j, val in enumerate((0.5, 1.0, -0.5)):
            ts(T.wb[:, 144 * j:144 * j + 144], T.jw[:], col(10), val, ALU.is_equal, ALU.mult, 72, ["jv", ("c", 10), "wb"], ["wb"])
    if CFG["dqa"]:
        act(col(9), col(7), AF.Identity, 1, [("c", 7)], [("c", 9)], bias=-M2048, scale=-4.0)
    for c in CFG["dei"]:
        add("V", lambda c=c: V.memset(T["wd%d" % c][:], 0.0), vc(224), (), [("w0", c)])
    for jh in range(2):
        act(col(13 + jh), cH, AF.Identity, 1, ["c0"], [("c", 13 + jh)], bias=jh - 1.0, scale=(1 - 2 * jh) / 16.0)
        for h in range(2):
            j = 2 * jh + h
            ts(T.pm[:, 128 * j:128 * j + 128], T.dj[:], 16.0 * (h - jh), col(13 + jh), ALU.is_equal, ALU.mult, 64, ["dj", ("c", 13 + jh)], [("pm", j)])
    act(col(15), cK, AF.Identity, 1, ["c0"], [("c", 15)], scale=16.0)
    act(T.lc[:, 0:4], T.lci[:, 0:4], AF.Identity, 4, ["lci", ("c", 15)], ["lc"], bias=col(15))
    act(col(18), cK, AF.Identity, 1, ["c0"], [("c", 18)], scale=592.0)
    ts(T.dk[:], T.dj[:], 0.0, col(18), ALU.is_equal, ALU.mult, 64, ["dj", ("c", 18)], ["dk"])
    act(col(19), cK, AF.Relu, 1, ["c0"], [("c", 19)], bias=-7.0, scale=0.5)
    ts(T.sel[:], T.jg[:], cG, col(19), ALU.is_equal, ALU.mult, 64, ["jg", "c0", ("c", 19)], ["sel"])
    ts(T.thf[:, 0:1], T.thi[:, 0:1], 0.5, 1024.0, ALU.mult, ALU.add, 1, ["thi"], ["thr"])
    act(T.thf[:, 1:2], T.thf[:, 0:1], AF.Identity, 1, ["thr"], ["th3"], bias=7.75)

    sent, stores, adds = [0], [], []
    for v in range(VI):
        for c in range(2):
            blk[0] = v * 2 + c
            U = {nm: T[nm + str(c)] for nm in OWN}

            def k_(*nms):
                return [(nm, c) for nm in nms]

            def ga(j, a, n, step=1):
                return U["ga"][:, j * LK + a:j * LK + a + n:step]

            def gt(j, a, n):
                return [("ga", c, j, u) for u in range(a // 128, (a + n) // 128)]

            def ab(ar, a, n, step=1):
                return U["ab"][:, ar * LK + a:ar * LK + a + n:step]

            def abt(ar, a=0, n=LK):
                return [("ab", c, ar, hf) for hf in range(a // 512, (a + n) // 512)]

            def ind(s, a, n):
                o = ocol(v, c, s) + a // 16
                return xw.indirect(T.off[:, o:o + n // 16])
            S1, S2, S3, S0 = [ps(U["sh"], j) for j in range(4)]
            a = ocol(v, c, 1)
            cp(ps(U["sh"], 0, 4), T.off[:, a:a + 4 * N], 2 * N, [("off", v, c, s) for s in range(4)], k_("sh"))
            PV, PB = CFG["pv"], CFG["pb"]
            a = 0
            for n in CFG["pa"]:
                act(ga(0, a, n), ind(0, a, n), AF.Identity, n * GATH, X + [("off", v, c, 0)], gt(0, a, n), scale=-1.0)
                a += n
            for s, pieces in zip(CFG["role"], PV):
                a = 0
                if (c, s) in CFG["dma"]:
                    for n in CFG["pd"]:
                        act(ga(s, a, n), ind(s, a, n), AF.Identity, n * GATH, X + [("off", v, c, s)], gt(s, a, n))
                        add("G", lambda o=ga(s, a, n), i=ga(0, a, n): g.dma_start(o, i, accum_op=ALU.add), CFG["dlat"], gt(0, a, n), gt(s, a, n),
                            sem=("d%d" % len(adds), 16, 16), hold=1000.0)
                        adds.append(a)
                        a += n
                    continue
                for n in pieces:
                    if (c, s, a // 512) in CFG["plain"]:
                        act(ga(s, a, n), ind(s, a, n), AF.Identity, n * GATH, X + [("off", v, c, s)], gt(s, a, n))
                        a += n
                        continue
                    tt(ga(s, a, n), ind(s, a, n), ga(0, a, n), ALU.add, n * GATH, X + [("off", v, c, s)] + gt(0, a, n), gt(s, a, n))
                    a += n
            done = [("CT", 0)]
            dei = c in CFG["dei"]
            mov = c in CFG["mov"]
            zero("pc", 0, 192 if dei or mov else 384, done + ["CO"])

            def sums(view, toks, p, rhs, last=False, kind=0):
                o, n = (0, 384) if p == 0 else (128 * (p - 1), 128)
                if mov:
                    for k0 in range(0, 16, 2 * CFG["rs"]):
                        w, end = [("CT", len(done))], last and k0 + 2 * CFG["rs"] == 16
                        mm([(ps(T.pc, (p + 2) % 3), T.wb[:, 144 * kind + 15 - k:144 * kind + 143 - k], view(k, 16), False, end and k == 15)
                            for k in range(k0, k0 + 2 * CFG["rs"])], ["wb"] + toks + (done if end else done[:1]), w, "pc")
                        done.extend(w)
                    return
                if dei:
                    o, n, rhs = o // 2, n // 2, T.gm[:, 0:48:2] if p == 0 else T.gm[:, 48:64:2]
                for k0 in range(0, 8, CFG["rs"]):
                    w, end = [("CT", len(done))], last and k0 + CFG["rs"] == 8
                    mm([(T.pc[:, o + k:o + n:8], view(k), rhs, False, end and k == 7) for k in range(k0, k0 + CFG["rs"])],
                       GM + toks + (done if end else done[:1]), w, "pc")
                    done.extend(w)

            def plain(p):
                return T.gm[:, 0:48] if p == 0 else T.gm[:, 48:64]
            for s in CFG["role"]:
                if (c, s) in CFG["relu"]:
                    for a in (0, 512):
                        ts(ab(s - 1, a, 512), ga(s, a, 512), 0.0, None, ALU.max, None, 256, gt(s, a, 512), abt(s - 1, a, 512))
                    sums(lambda k, st=8: ga(s, k, LK - k, st), gt(s, 0, LK), s - 1, T.gm[:, 0:16], kind=2)
                    sums(lambda k, st=8: ab(s - 1, k, LK - k, st), abt(s - 1), s - 1, T.gm[:, 32:48], kind=1)
                else:
                    for a in range(0, LK, PB):
                        if (c, s, a // 512) in CFG["plain"]:
                            bk = "pd%d" % (a // 512)
                            for u in (0, s):
                                lin(bk, [(T[bk][:, 0:512], IB, ga(u, a, 512))], ["ib+"] + gt(u, a, 512), [bk], u == 0, u == s)
                            act(ab(s - 1, a, 512), T[bk][:, 0:512], AF.Abs, 512, [bk], abt(s - 1, a, 512), [bk])
                        elif dei:
                            act(ab(s - 1, a, 512), ga(s, a // 512, LK - a // 512, 2), AF.Abs, 512, gt(s, 0, LK), abt(s - 1, a, 512))
                        else:
                            act(ab(s - 1, a, PB), ga(s, a, PB), AF.Abs, PB, gt(s, a, PB), abt(s - 1, a, PB))
                    sums(lambda k, st=8: ab(s - 1, k, LK - k, st), abt(s - 1), s - 1, plain(s - 1))
            for j, (s, t) in enumerate(CFG["pairs"][c]):
                for hf in range(2):
                    bk, a = "pd%d" % hf, 512 * hf
                    terms = [(m, 0) for m, u in ((IB, s), (NB, t)) if (c, u, hf) in CFG["plain"]] + [(IB, s), (NB, t)]
                    for m, u in terms:
                        lin(bk, [(T[bk][:, 0:512], m, ga(u, hf, LK - hf, 2) if dei else ga(u, a, 512))],
                            ["ib+", "ib-"] + (gt(u, 0, LK) if dei else gt(u, a, 512)), [bk], u == terms[0][1], u == t)
                    act(ab(3 + j, a, 512), T[bk][:, 0:512], AF.Abs, 512, [bk], abt(3 + j, a, 512), [bk])
                sums(lambda k, st=8: ab(3 + j, k, LK - k, st), abt(3 + j), 5 - s - t, plain(5 - s - t), j == 2)
            S23 = ps(U["sh"], 1, 2)
            IHS = ["ih+", "ih-"] + k_("sh")
            mm([(ps(T.r1, 0), IH, S2, True, False), (ps(T.r1, 0), NH, S1, False, True), (ps(T.r1, 1), IH, S2, True, False), (ps(T.r1, 1), NH, S3, False, True)],
               IHS, ["R1"], "r1")
            if dei:
                cp(U["wd"][:, 2:386:2], T.pc[:, 0:192], 192, done + k_("w0"), k_("wt"), ["pc"])
                mm([(ps(T.pc, p), U["wd"][:, 2 - e + 128 * p:130 - e + 128 * p], ps(T.ih, e), e == 0, e == 1) for p in range(3) for e in range(2)],
                   k_("wt") + ["ih+"], ["CO"] + done, "pc")
            elif not mov:
                tt(U["wt"][:], T.pc[:, 0:384], T.wm[:], ALU.mult, 384, done + ["wm"], k_("wt"), ["pc"])
                mm([(ps(T.pc, p), ps(U["wt"], 2 * p, 2), T.em[:], True, True) for p in range(3)], k_("wt") + ["em"], ["CO"] + done, "pc")
            CO, nch = (done, 3) if mov else (["CO"], 2)
            cp(ps(U["ch"], 0, nch), ps(T.pc, 0, nch), nch * N, CO, k_("ch"), ["pc"])
            act(ps(T.r1, 4), ps(T.pc, 2), AF.Identity, N, CO + ["thr"], ["Y"], ["pc", "r1"], bias=T.thf[:, 0:1], scale=-1.0 if mov else -0.5)
            lin("pk", [(ps(T.pk, 0, 4), T.ka[0:2, :], T.kb[0:2, :])], ["ka", ("kb", 1), ("kb", 2)], ["K"], True)
            terms = [(T.zm[:, 256:384], T.zm[:, 384:512], 2), (NH, NH, 2)] * mov
            lin("pk", [(ps(T.pk, 2 * p + e), m[e], ps(U["ch"], u)) for p in range(2) for e in range(2)
                       for *m, u in terms[:1] + [(T.zm[:, 0:128], T.zm[:, 128:256], p), (IH, IH, p)] + terms[1:]],
                [("zm", j) for j in range(4 if mov else 2)] + ["ih+", "ih-"] + k_("ch"), ["K"], False, True)
            ts(U["m1"][:], ps(T.pk, 0, 2), OFFK + 1024.0, None, ALU.min, None, 128, ["K"], k_("m1"), ["pk"])
            tt(U["mk"][:], ps(T.pk, 2, 2), U["m1"][:], ALU.min, 128, ["K"] + k_("m1"), k_("mk"), ["pk"])
            ts(U["tk"][:], U["mk"][:], 8191, None, ALU.bitwise_and, None, 128, k_("mk"), k_("tk"))
            tt(U["dt"][:], ps(U["tk"], 0), ps(U["tk"], 1), ALU.subtract, 128, k_("tk"), k_("dt"))
            if c in CFG["dqa"]:
                act(U["uu"][:], U["dt"][:], AF.Identity, N, k_("dt"), k_("uu"), bias=M2048)
                act(ps(T.pk, 4), U["uu"][:], AF.Identity, N, k_("uu") + [("c", 9)], ["DQ"], ["pk"], bias=col(9))
            else:
                ts(ps(T.pk, 4), U["dt"][:], M2048, col(8), ALU.add, ALU.subtract, N, k_("dt") + [("c", 8)], ["DQ"], ["pk"])
            tt(U["dq"][:], U["dt"][:], ps(T.pk, 4), ALU.subtract, N, k_("dt") + ["DQ"], k_("dq"), ["pk"])
            turn(U["dv"][:], U["dq"][:], k_("dq"), k_("dv"))
            scan(U["uu"][:, ::-1], U["dv"][:, ::-1], T.one[:], ALU.add, ALU.min, k_("dv") + ["one"], k_("uu"))
            scan(U["rt"][:], U["uu"][:], T.kp3[:], ALU.max, ALU.min, k_("uu") + ["kp3"], k_("rt"))
            turn(ps(T.pk, 5), U["rt"][:], k_("rt"), ["RT"], ["pk"])
            tt(ps(T.pk, 6), ps(T.pk, 5), U["dt"][:], ALU.mult, N, ["RT"] + k_("dt"), ["KK"], ["pk"])
            tt(U["tf"][:], ps(U["tk"], 0), ps(T.pk, 6), ALU.subtract, N, ["KK"] + k_("tk"), k_("tf"), ["pk"])
            act(U["junk"][:], ps(T.pk, 6), AF.Sign, N, ["KK"], k_("junk"), ["pk"])
            if v < VI - 1:
                act(ps(T.r2, 4), U["junk"][:], AF.Abs, N + 135, k_("junk"), ["SW"] + k_("cnt"), ["r2"], accum_out=T.cnt[:, c:c + 1])
            else:
                act(ps(T.r2, 4), U["junk"][:], AF.Abs, N, k_("junk"), ["SW"], ["r2"])
            act(ps(T.r2, 5), U["junk"][:], AF.Abs, N, k_("junk"), ["SW2"], ["r2"])
            if c == 1 and v < VI - 1:
                n2, n3, n4, n5 = [T.cnt[:, u:u + 1] for u in (2, 3, 4, 5)]
                act(T.lc[:, 4:6], T.cnt[:, 0:2], AF.Identity, 2, [("cnt", 0), ("cnt", 1)], ["cb"])
                mm([(T.pk[:, 448:449], T.sel[:], T.lc[:, 4 + u:5 + u], u == 0, u == 1) for u in range(2)], ["sel", "cb"], ["CN"], "pk")
                act(n2, T.pk[:, 448:449], AF.Identity, 1, ["CN"], ["n2"], ["pk"], bias=-7.75)
                act(n3, n2, AF.Identity, 1, ["n2"], ["n3"], bias=M16)
                act(n4, n3, AF.Identity, 1, ["n3"], ["n4"], bias=M16, scale=-1.0)
                act(n5, n4, AF.Identity, 1, ["n4", "n2"], ["n5"], bias=n2)
                act(T.thf[:, 0:1], n5, AF.Identity, 1, ["n5", "th3"], ["thr"], bias=T.thf[:, 1:2])
            lin("r2", [(ps(T.r2, 2, 2), I16, S23)], IHS + ["i16+"], ["R2"], True)
            ts(ps(U["fm"], 0), U["tf"][:], 2048.0, None, ALU.is_lt, None, N, k_("tf"), k_("f0"))
            ts(ps(U["fm"], 1), U["tf"][:], 4096.0, None, ALU.is_ge, None, N, k_("tf"), k_("f2"))
            ts(U["xf"][:], U["tf"][:], 2047, None, ALU.bitwise_and, None, N, k_("tf"), k_("xf"))
            tt(U["ov"][:], U["xf"][:], ps(T.r1, 4), ALU.is_gt, N, k_("xf") + ["Y"], k_("ov"), ["r1"])
            FM = k_("f0", "f2")
            scan(U["run"][:], T.keep[:], U["rt"][:], ALU.mult, ALU.add, k_("rt") + ["keep"], k_("run"))
            lin("pl", [(T.pl[:, 0:4], IB, T.lc[:, 0:4])], ["ib+", "lc"], ["L"], True)
            lin("pl", [(T.pl[:, 2 * jh:2 * jh + 2], T.pm[:, 128 * (2 * jh + h):128 * (2 * jh + h) + 128], U["run"][:, 16 * h + 15:N:32])
                       for jh in range(2) for h in range(2)], [("pm", j) for j in range(4)] + k_("run"), ["L"], False, True)
            lc, xc = T.lst[:, 4 * c:4 * c + 4], T.xs[:, LK * c:LK * c + LK]
            cp(lc, T.pl[:, 0:4], 4, ["L"], k_("lst"), ["pl"])
            if c in CFG["bwv"]:
                act(U["bu"][:], ga(0, 0, LK).indirect(lc), AF.Identity, N * GATH, k_("lst") + gt(0, 0, LK), k_("bu"), bias=191.75, scale=-0.5)
                act(U["bv"][:], xc.indirect(lc), AF.Identity, N * GATH, k_("lst") + [X[c]], k_("bv"), scale=0.5)
                tt(U["bw"][:], U["bu"][:], U["bv"][:], ALU.add, 2 * N, k_("bu", "bv"), k_("bw"))
            else:
                act(ps(U["bb"], 0), ga(0, 0, LK).indirect(lc), AF.Identity, N * GATH, k_("lst") + gt(0, 0, LK), k_("bu"), scale=-1.0)
                act(ps(U["bb"], 1), xc.indirect(lc), AF.Identity, N * GATH, k_("lst") + [X[c]], k_("bv"))
            for u in range(2 * c):
                if u not in CFG["bwv"]:
                    bk = "pd%d" % u
                    lin(bk, [(ps(T[bk], 0), IB, ps(T["bb%d" % u], e)) for e in range(2)], ["ib+", ("bu", u), ("bv", u)], [bk], True, True)
                    act(T["bw%d" % u][:], ps(T[bk], 0), AF.Identity, N, [bk], [("bw", u)], [bk], bias=191.75, scale=0.5)
                tt(T.xs[:, LK * u:LK * u + LK].indirect(T.lst[:, 4 * u:4 * u + 4]), T["bw%d" % u][:], T.m192[:], ALU.add, N * CFG["scat"],
                   [("lst", u), ("bw", u), "m192"], [X[u]])
            t0, t1, d1, d2, e1, e2, q0, q2 = [ps(U[b], j) for b in ("tq", "dd", "ee", "qq") for j in range(2)]
            zero("r3", 0, 256, ["R3"])
            lin("r3", [(ps(T.r3, j), IH, (S0, S1)[j % 2]) for j in range(4)], IHS, ["R3"])
            tt(U["tq"][:], ps(T.r1, 0, 2), U["fm"][:], ALU.mult, 128, ["R1"] + FM, k_("tq"), ["r1"])
            TQ = IHS + k_("tq")
            mm([(ps(T.pl, 1), IH, S0, True, True), (ps(T.pl, 2), IH, S1, True, False)], IHS, ["RA"], "pl")
            lin("pl", [(ps(T.pl, 2), IH, t0)], TQ, ["RA"], False, True)
            lin("r2", [(ps(T.r2, 2), N16, t0), (ps(T.r2, 2), N16, t1), (ps(T.r2, 3), I16, t1), (ps(T.r2, 2), T.dk[:], U["ov"][:]), (ps(T.r2, 3), T.dk[:], U["ov"][:])],
                TQ + ["i16+", "i16-", "dk"] + k_("ov"), ["R2"], False, True)
            lin("r2", [(ps(T.r2, 0, 2), IH, S23), (ps(T.r2, 0), NH, t0), (ps(T.r2, 0), NH, t1), (ps(T.r2, 1), IH, t1)], TQ, ["R2"], True, True)
            lin("r3", [(ps(T.r3, 1), IH, t0), (ps(T.r3, 3), IH, t0)], TQ, ["R3"])
            zero("r1", 128, 128, ["R1"])
            lin("r1", [(ps(T.r1, 2 + e), m, x) for e in range(2) for m, x in ((IH, S0), (NH, S1), (NH, t0))], TQ, ["R1"])
            for e in range(2):
                tt(ps(U["ao"], e), ps(T.pl, 1 + e), U["ov"][:], ALU.mult, N, ["RA"] + k_("ov"), k_("ao%d" % e), ["pl"])
            tt(U["pr"][:], ps(T.r2, 0, 2), U["ao"][:], ALU.mult, 128, ["R2"] + k_("ao0", "ao1"), k_("pr"), ["r2"])
            tt(U["zi"][:], ps(T.r2, 2, 2), U["pr"][:], ALU.add, 128, ["R2"] + k_("pr"), k_("zi"), ["r2"])
            ts(U["bn"][:], U["zi"][:], 4, 2047, ALU.arith_shift_right, ALU.bitwise_and, 128, k_("zi"), k_("bn"))
            tt(U["dd"][:], U["bn"][:], ps(T.pl, 1, 2), ALU.subtract, 128, k_("bn") + ["RA"], k_("dd"), ["pl"])
            lin("r1", [(ps(T.r1, 2), IH, d1), (ps(T.r1, 3), IH, d1), (ps(T.r1, 3), NH, d2)], IHS + k_("dd"), ["R1"])
            lin("r3", [(ps(T.r3, 2, 2), IH, U["dd"][:])], IHS + k_("dd"), ["R3"])
            tt(U["ee"][:], ps(T.r2, 4, 2), U["dd"][:], ALU.mult, 128, ["SW", "SW2"] + k_("dd"), k_("ee"), ["r2"])
            E = IHS + k_("ee")
            lin("r1", [(ps(T.r1, 2), NH, e1), (ps(T.r1, 2), NH, e2), (ps(T.r1, 3), NH, e1), (ps(T.r1, 3), IH, e2)], E, ["R1"], False, True)
            lin("r3", [(ps(T.r3, 0, 2), IH, U["ee"][:]), (ps(T.r3, 2, 2), NH, U["ee"][:])], E, ["R3"])
            tt(U["qq"][:], ps(T.r1, 2, 2), U["fm"][:], ALU.mult, 128, ["R1"] + FM, k_("qq"), ["r1"])
            lin("r3", [(ps(T.r3, 1), IH, q0), (ps(T.r3, 2), NH, q0), (ps(T.r3, 2), NH, q2), (ps(T.r3, 3), IH, q2)], IHS + k_("qq"), ["R3"], False, True)
            ob = ocol(v + 1, c, 0)
            cp(T.off[:, ob:ob + 4 * N], ps(T.r3, 0, 4), 4 * N, ["R3"], [("off", v + 1, c, 0)], ["r3"])
            trs = [[], []]
            for s in (1, 2, 3):
                hop, rel, mask, call = rt[(rank, s)]
                rid, pid = topo.addr(hop, core)
                a = ocol(v + 1, c, s)
                trs[call].append(RemoteDMATransfer(dst_ids=[DstId(rid=rid, pnc=pid)], dma_engine_mask=mask, remote_sem=T.sem["a%d_%d_%d" % (v, c, s)],
                                                   src=T.off[:, ob + s * N:ob + (s + 1) * N], dst=T.off[:, a:a + N]))
                sent[0] += bits(mask)
            snd = add("G", lambda trs=trs: [g.remote_dma_fused(t, local_sem=T.sem.sent) for t in trs], 1000.0, [("off", v + 1, c, 0)], (), sem=("", 0, 0))
            for s in (1, 2, 3):
                r0 = (rank - STEP[s]) % NR
                hop, rel, mask, call = rt[(r0, s)]
                cntv = bits(mask) if rel is None else bits(topo.mask(rel, core))
                add("N", None, CFG["net"][s] + (CFG["once"] if v == c == 0 else 0.0), (), [("off", v + 1, c, s)], sem=("a%d_%d_%d" % (v, c, s), cntv, 0), after=[snd])
            if v < VI - 1:
                pass
            else:
                if c == 1:
                    stores.append(dma("S", T.yx[:], T.xs[:], "st", 0, X, ()))
                for s in (0,) + CFG["role"]:
                    a, y = ocol(VI, c, s), TT * s + N * c
                    cp(T.ysf[:, y:y + N], T.off[:, a:a + N], N, [("off", VI, c, s)], [("ys", c, s)])
                    stores.append(dma("SA"[s % 2], T.ys[:, y:y + N], T.ysf[:, y:y + N], "st", 0, [("ys", c, s)], ()))
    return ops, sent[0], 16 * len(stores)


def emit(g, T, ops, order, sent, stored):
    queue = {"V": g.vector, "A": g.scalar, "P": g.tensor, "G": g, "S": g.sync}
    csem = {"V": "cv", "A": "ca", "P": "cp", "G": "cg"}
    mark, total = {}, {}
    for q in order:
        k = 0
        for i in order[q]:
            if ops[i]["sem"] is None:
                k += 1
                mark[i] = (csem[q], k, 1)
            else:
                mark[i] = ops[i]["sem"]
        if k:
            total[csem[q]] = k
    for q in queue:
        seen = {}
        for i in order.get(q, ()):
            need = {}
            for d in ops[i]["deps"]:
                if q == "P" and ops[d]["q"] == "P":
                    continue
                s, val, inc = mark[d]
                need[s] = max(need.get(s, 0), val)
            for s in need:
                if need[s] > seen.get(s, 0):
                    queue[q].wait_ge(T.sem[s], need[s])
                    seen[s] = need[s]
            ins = ops[i]["fn"]()
            s, val, inc = mark[i]
            if s:
                ins.then_inc(T.sem[s], inc)
    for s in total:
        g.wait_ge(T.sem[s], total[s])
    g.wait_ge(T.sem.sent, sent)
    g.wait_ge(T.sem.st, stored)


def rank_program(g, core, T, topo):
    rt = routes(T, topo)
    rank = T.rank_of(core)
    if rank is not None:
        ops, sent, stored = build(g, core, T, topo, rank, rt)
        if "order" not in _PLAN:
            cases, mid = [(ops, CFG["ls"], CFG["lx"])], dict(CFG)
            for case in CFG["cases"]:
                CFG.update(case)
                cases.append((build(g, core, T, topo, rank, rt)[0], CFG["ls"], CFG["lx"]))
                CFG.update(mid)
            _PLAN["order"], _PLAN["end"] = min([schedule(cases, seed) for seed in CFG["seeds"]], key=lambda plan: plan[1])
            _PLAN["ops"] = ops
        emit(g, T, ops, _PLAN["order"], sent, stored)
        return
    for (r, s), (hop, rel, mask, call) in rt.items():
        if rel == core:
            dst = T.cores[(r + STEP[s]) % NR]
            rid, pid = topo.addr(dst, core)
            m2 = topo.mask(core, dst)
            for v in range(VI):
                for c in range(2):
                    a = ocol(v + 1, c, s)
                    sem = T.sem["a%d_%d_%d" % (v, c, s)]
                    g.wait_ge(sem, bits(mask))
                    g.remote_dma(T.off[:, a:a + N], T.off[:, a:a + N], sem, T.sem.sent, pid, rid, m2)
            g.wait_ge(T.sem.sent, bits(m2) * VI * 2)
